import numpy as np
import ml_dtypes


def mxq(x, axis, fmt="e4m3"):
    dtype, down = {"e4m3": (ml_dtypes.float8_e4m3fn, 7), "e5m2": (ml_dtypes.float8_e5m2, 14)}[fmt]
    v = np.moveaxis(np.asarray(x, np.float32).astype(ml_dtypes.bfloat16).astype(np.float64), axis, -1)
    blocks = v.reshape(v.shape[:-1] + (-1, 32))
    amax = np.abs(blocks).max(-1, keepdims=True)
    byte = np.maximum(np.where(amax > 0, np.frexp(amax)[1] - 1 + 127, 0) - down, 1)
    scale = np.exp2(byte - 127.0)
    codes = (blocks / scale).astype(np.float32).astype(dtype).astype(np.float64)
    return np.moveaxis((codes * scale).reshape(v.shape), -1, axis)


WIDE = False


def mx_kscale(k):
    if not WIDE:
        return np.ones(k)
    levels = np.array([10, -10, 5, -5, 0])
    if k % 512:
        return np.exp2(np.random.permutation(np.resize(levels, k // 32))).repeat(32)
    a = np.empty((k // 512, 16))
    for p in range(k // 512):
        a[p, :8] = np.random.permutation(np.resize(levels, 8))
        for g in range(8):
            far = levels[np.abs(levels - a[p, g]) >= 10]
            a[p, g + 8] = far[np.random.randint(len(far))]
    return np.exp2(a.ravel()).repeat(32)


def f64(x):
    return np.asarray(x).astype(np.float64)


def striped(idx):
    return np.tile(idx.reshape(-1, 16).T, (8, 1)).astype(np.uint16)


def unstriped(offs):
    return offs[:16].T.reshape(-1).astype(np.int64)


def striped8(idx):
    return np.concatenate([x.reshape(-1, 16).T for x in idx]).astype(np.uint16)


def runs(offs, k):
    lists = np.stack([offs[16 * r : 16 * r + 16].T.reshape(-1) for r in range(8)]).astype(np.int64)
    return lists[np.arange(k) % 512 // 64]


def pack_weight(w):
    k, n = w.shape
    w = f64(np.asarray(w, np.float32).astype(ml_dtypes.bfloat16)).reshape(k // 32, 32, n)
    amax = np.abs(w).max(1)
    byte = np.clip(np.where(amax > 0, np.frexp(amax)[1] - 1 + 127 - 7, 1), 1, 254)
    scaled = (w * np.exp2(127.0 - byte)[:, None, :]).reshape(k, n).astype(np.float32)
    words = np.ascontiguousarray(scaled.reshape(k // 512, 128, 4, n).transpose(0, 1, 3, 2)).astype(ml_dtypes.float8_e4m3fn).view(np.uint8)
    return words, np.ascontiguousarray(byte.astype(np.uint8).reshape(k // 512, 16, n))


def unpack_weight(words, scales):
    g, p, n, _ = words.shape
    vals = np.ascontiguousarray(words).view(ml_dtypes.float8_e4m3fn).astype(np.float64) * np.repeat(np.exp2(scales.astype(np.float64) - 127.0), 8, axis=1)[..., None]
    return vals.transpose(0, 1, 3, 2).reshape(g * 512, n)


def sigmoid(v):
    return 1.0 / (1.0 + np.exp(-np.maximum(v, -700.0)))

def planes(y):
    n, m = y.shape
    v = y.astype(np.float32).astype(ml_dtypes.bfloat16).astype(np.float64).reshape(n // 32, 32, m)
    top = np.abs(v).max(1)
    byte = np.clip(np.where(top > 0, np.frexp(top)[1] - 1 + 127 - 7, 1), 1, 254)
    codes = (v * np.exp2(127.0 - byte)[:, None, :]).reshape(n, m).astype(np.float32).astype(ml_dtypes.float8_e4m3fn).view(np.uint8)
    words = codes.reshape(n // 512, 128, 4, m).transpose(0, 1, 3, 2)
    return np.ascontiguousarray(words), np.ascontiguousarray(byte.astype(np.uint8).reshape(n // 512, 16, m))


K, T, S, N, G, H, W = 512, 1024, 512, 512, 2048, 512, 256


def setup_inputs():
    n = np.random.standard_normal
    s = mx_kscale(K)[:, None]
    u = mx_kscale(S)
    packed_xT = pack_weight(n((K, T)) * s)
    packed_dT = pack_weight(n((K, G)) / s)
    packed_w1 = pack_weight(n((H, N)) / np.sqrt(2 * H) / u[:, None])
    packed_w2 = pack_weight(n((H, N)) / np.sqrt(2 * H) / u[:, None])
    perm = np.stack([np.random.permutation(S) for _ in range(8)])
    return {
        "x_words": packed_xT[0],
        "x_scales": packed_xT[1],
        "d_words": packed_dT[0],
        "d_scales": packed_dT[1],
        "gn": (np.random.uniform(0.5, 1.5, (H, 1)) * u[:, None]).astype(np.float32),
        "gm": (np.random.uniform(0.5, 1.5, (H, 1)) * u[:, None]).astype(np.float32),
        "w1_words": packed_w1[0],
        "w1_scales": packed_w1[1],
        "w2_words": packed_w2[0],
        "w2_scales": packed_w2[1],
        "offs": striped(np.random.permutation(T)[:S]),
        "k1": striped8(np.random.randint(0, G, (8, H))),
        "two": striped(np.random.permutation(T)[:S]),
        "n1": striped8(perm[:, :W]),
        "n2": striped8(perm[:, W:]),
        "n3": striped8(np.stack([np.random.permutation(S) for _ in range(8)])),
        "n4": striped8(np.stack([np.random.permutation(S) for _ in range(8)])),
        "n5": striped(np.random.randint(0, S, G)),
    }


def reference(x_words, x_scales, d_words, d_scales, gn, gm, w1_words, w1_scales, w2_words, w2_scales, offs, k1, two, n1, n2, n3, n4, n5):
    d_k1 = unpack_weight(d_words, d_scales)[np.arange(K)[:, None], runs(k1, K)]
    xq = unpack_weight(x_words, x_scales)[:, unstriped(offs)]
    a = 0.0625 * (d_k1.T @ xq)
    pb = a[np.arange(H)[:, None], runs(n2, H)]
    pa = a[np.arange(H)[:, None], runs(n1, H)]
    rb = pb * sigmoid(pb - pa)
    ra = pa * sigmoid(pa - pb)
    ds = np.zeros((H, S))
    ds[np.arange(H)[:, None], runs(n1, H)] = ra
    dt = ds.copy()
    dt[np.arange(H)[:, None], runs(n2, H)] = rb
    z = f64(gn) * dt
    x_two = unpack_weight(x_words, x_scales)[:, unstriped(two)]
    b = 0.0625 * (d_k1.T @ x_two)
    z2 = f64(gm) * (np.minimum(np.maximum(b, b[np.arange(H)[:, None], runs(n3, H)]), b[np.arange(H)[:, None], runs(n4, H)]))
    h = unpack_weight(w1_words, w1_scales).T @ mxq(z, 0, "e4m3") + unpack_weight(w2_words, w2_scales).T @ mxq(z2, 0, "e4m3")
    mb = h[:, unstriped(n5)]
    mx = mb.reshape(N, S, 4).max(axis=2)
    mn = mb.reshape(N, S, 4).min(axis=2)
    out_0 = mx * np.tanh(h - mn)
    return (out_0,) + planes(out_0)

@@ -1,0 +1,278 @@
+from contextlib import ExitStack
+
+import concourse.mybir as mybir
+
+K, T, S, N, G, H, W = 512, 1024, 512, 512, 2048, 512, 256
+FLOPS = 4 * 2 * 512 * 512 * 512
+
+F32 = mybir.dt.float32
+BF16 = mybir.dt.bfloat16
+I32 = mybir.dt.int32
+U32 = mybir.dt.uint32
+U16 = mybir.dt.uint16
+U8 = mybir.dt.uint8
+FP8X4 = mybir.dt.float8_e4m3fn_x4
+ALU = mybir.AluOpType
+ACT = mybir.ActivationFunctionType
+
+P = 128
+PACK = 4
+CHUNKS = (128,128,128,128)
+SPARE = 16
+MEMBERS = 4
+
+
+def tile_picked_kjduelminmxgtan_none_po_kernel(
+    tc, x_words, x_scales, d_words, d_scales, gn, gm, w1_words, w1_scales, w2_words, w2_scales,
+    offs, k1, two, n1, n2, n3, n4, n5, out_0, out_1, out_2,
+):
+    nc = tc.nc
+
+    def words_in_hbm(words):
+        return words[0].rearrange("p c r -> p (c r)").bitcast(I32)
+
+    with ExitStack() as ctx:
+        lists = ctx.enter_context(tc.tile_pool(name="lists", bufs=1))
+        keep = ctx.enter_context(tc.tile_pool(name="keep", bufs=1))
+        work = ctx.enter_context(tc.tile_pool(name="work", bufs=4))
+        psum = ctx.enter_context(tc.psum_pool(name="psum", bufs=1))
+
+        def load_list(source, name):
+            tile = lists.tile(list(source.shape), U16, name=name)
+            nc.sync.dma_start(tile[:], source)
+            return tile
+
+        def deal(out, in_):
+            nc.vector.tensor_copy(out.rearrange("p (t m) -> p t m", t=PACK), in_.rearrange("p (m t) -> p t m", t=PACK))
+
+        d_bytes = keep.tile([P, G], U8, name="d_bytes", align_bytes=64)
+        x_bytes = keep.tile([P, T], U8, name="x_bytes", tag="bytes_in", align_bytes=64)
+        nc.gpsimd.memset(d_bytes[:].bitcast(I32), 0)
+        nc.gpsimd.memset(x_bytes[:].bitcast(I32), 0)
+        k1_l = load_list(k1, "k1_l")
+        offs_l = load_list(offs, "offs_l")
+        for e in range(2):
+            nc.sync.dma_start(d_bytes[e:P:16, :].bitcast(I32), d_scales[0, e:16:2, :].bitcast(I32))
+        x_table = keep.tile([P, T], I32, name="x_table", align_bytes=64)
+        nc.sync.dma_start(x_table[:], words_in_hbm(x_words))
+        d_table = keep.tile([P, G], I32, name="d_table", tag="words_in", align_bytes=64)
+        nc.sync.dma_start(d_table[:], words_in_hbm(d_words))
+        for q in range(4):
+            nc.sync.dma_start(x_bytes[32 * q : 32 * q + 4, :].bitcast(I32), x_scales[0, 4 * q : 4 * q + 4, :].bitcast(I32))
+        two_l = load_list(two, "two_l")
+        n1_l = load_list(n1, "n1_l")
+        n2_l = load_list(n2, "n2_l")
+        n3_l = load_list(n3, "n3_l")
+        n4_l = load_list(n4, "n4_l")
+        n5_l = load_list(n5, "n5_l")
+        gn_t = keep.tile([P, PACK], F32, name="gn_t")
+        gm_t = keep.tile([P, PACK], F32, name="gm_t")
+        nc.gpsimd.dma_start(gn_t[:], gn.rearrange("(p t) o -> p (t o)", t=PACK))
+        nc.gpsimd.dma_start(gm_t[:], gm.rearrange("(p t) o -> p (t o)", t=PACK))
+
+        h_rows = [keep.tile([P, S + SPARE], F32, name="h_rows%d" % t) for t in range(PACK)]
+        for t in range(PACK):
+            nc.gpsimd.memset(h_rows[t][:, S:], 0.0)
+
+        key_bytes_raw = keep.tile([P, H], U8, name="key_bytes_raw", align_bytes=64)
+        key_bytes = keep.tile([P, H], U8, name="key_bytes", align_bytes=64)
+        nc.vector.tensor_copy(key_bytes_raw[:], d_bytes[:].indirect(k1_l[:]))
+        deal(key_bytes[:], key_bytes_raw[:])
+        for e in range(2):
+            nc.scalar.dma_start(key_bytes[2 + e : P : 32, :].bitcast(I32), key_bytes[16 + e : P : 32, :].bitcast(I32))
+
+        def pick_tokens(offsets, name):
+            words = keep.tile([P, S], U32, name=name + "_words", align_bytes=64)
+            scales = keep.tile([P, S], U8, name=name + "_bytes", align_bytes=64)
+            nc.vector.tensor_copy(words[:], x_table[:].bitcast(U32).indirect(offsets[:]))
+            nc.vector.tensor_copy(scales[:], x_bytes[:].indirect(offsets[:]))
+            return words, scales
+
+        xa_words, xa_bytes = pick_tokens(offs_l, "xa")
+        key_words_raw = keep.tile([P, H], U32, name="key_words_raw", align_bytes=64)
+        key_words = keep.tile([P, H], U32, name="key_words", align_bytes=64)
+        nc.vector.tensor_copy(key_words_raw[:], d_table[:].bitcast(U32).indirect(k1_l[:]))
+        deal(key_words[:], key_words_raw[:])
+
+        def scores(words, scales, name):
+            banks = []
+            for t in range(PACK):
+                bank = psum.tile([P, S], F32, name="%s%d" % (name, t))
+                cols = slice(P * t, P * (t + 1))
+                nc.tensor.matmul_mx(
+                    bank[:], lhsT=key_words[:, cols].bitcast(FP8X4), lhsT_scale=key_bytes[:, cols],
+                    rhs=words[:].bitcast(FP8X4), rhs_scale=scales[:], start=True, stop=True,
+                )
+                banks.append(bank)
+            return banks
+
+        a_banks = scores(xa_words, xa_bytes, "bank_a")
+        xb_words, xb_bytes = pick_tokens(two_l, "xb")
+        b_banks = scores(xb_words, xb_bytes, "bank_b")
+
+        w_table = keep.tile([P, 2, N], I32, name="w_table", tag="words_in", align_bytes=64)
+        nc.sync.dma_start(w_table[:, 0, :], words_in_hbm(w1_words))
+        nc.sync.dma_start(w_table[:, 1, :], words_in_hbm(w2_words))
+        w_bytes_raw = keep.tile([P, N], U8, name="w_bytes_raw", tag="bytes_in", align_bytes=64)
+        nc.gpsimd.memset(w_bytes_raw[:].bitcast(I32), 0)
+        for j, scales in enumerate((w1_scales, w2_scales)):
+            for q in range(4):
+                rows = slice(32 * q + 4 * j, 32 * q + 4 * j + 4)
+                nc.sync.dma_start(w_bytes_raw[rows, :].bitcast(I32), scales[0, 4 * q : 4 * q + 4, :].bitcast(I32))
+
+        z_pairs = [keep.tile([P, 2, S, 2], BF16, name="z_pairs%d" % j, align_bytes=64) for j in range(2)]
+        z_codes = [keep.tile([P, S], U32, name="z_codes%d" % j, align_bytes=64) for j in range(2)]
+        z_bytes = [keep.tile([P, S], U8, name="z_bytes%d" % j, align_bytes=64) for j in range(2)]
+
+        def round_rows(on_vector, j, t, values, gain):
+            out = z_pairs[j][:, t // 2, :, t % 2]
+            if on_vector:
+                nc.vector.tensor_scalar(out, values, gain[:, t : t + 1], None, ALU.mult)
+            else:
+                nc.scalar.activation(out, values, ACT.Copy, scale=gain[:, t : t + 1])
+
+        def quantize_rows(on_vector, j):
+            grouped = keep.tile([P, S, 2], U32, name="z_grouped%d" % j, align_bytes=64)
+            pairs = z_pairs[j][:].rearrange("p u s e -> p u (s e)")
+            if on_vector:
+                nc.vector.tensor_copy(grouped[:].bitcast(I32), pairs.bitcast(I32).rearrange("p u s -> p s u"))
+            else:
+                nc.scalar.copy(grouped[:], pairs.bitcast(U32).rearrange("p u s -> p s u"))
+            nc.vector.quantize_mx(
+                z_codes[j][:].bitcast(FP8X4), z_bytes[j][:], grouped[:].rearrange("p s u -> p (s u)").bitcast(BF16)
+            )
+
+        def duel_pick(t):
+            a_rows = work.tile([P, S], F32, name="a_rows", bufs=4)
+            nc.scalar.activation(a_rows[:], a_banks[t][:], ACT.Copy, scale=0.0625)
+            pa = work.tile([P, W], F32, name="pa")
+            pb = work.tile([P, W], F32, name="pb")
+            nc.scalar.activation(pa[:], a_rows[:].indirect(n1_l[:]), ACT.Copy)
+            nc.scalar.activation(pb[:], a_rows[:].indirect(n2_l[:]), ACT.Copy)
+            gap = work.tile([P, W], F32, name="gap")
+            nc.vector.tensor_tensor(gap[:], pb[:], pa[:], ALU.subtract)
+            return pa, pb, gap
+
+        def duel_put(pa, pb, gap):
+            half = work.tile([P, W], F32, name="half")
+            nc.scalar.activation(half[:], gap[:], ACT.Tanh, scale=0.5)
+            share_a = work.tile([P, W], F32, name="share_a")
+            share_b = work.tile([P, W], F32, name="share_b")
+            nc.vector.tensor_scalar(share_a[:], half[:], -0.5, 0.5, ALU.mult, ALU.add)
+            nc.vector.tensor_scalar(share_b[:], half[:], 0.5, 0.5, ALU.mult, ALU.add)
+            dt_rows = work.tile([P, S], F32, name="dt_rows")
+            nc.vector.tensor_tensor(dt_rows[:].indirect(n1_l[:]), pa[:], share_a[:], ALU.mult)
+            nc.vector.tensor_tensor(dt_rows[:].indirect(n2_l[:]), pb[:], share_b[:], ALU.mult)
+            return dt_rows
+
+        def clip(t):
+            b_rows = work.tile([P, S], F32, name="b_rows", bufs=4)
+            nc.scalar.activation(b_rows[:], b_banks[t][:], ACT.Copy, scale=0.0625)
+            b3 = work.tile([P, S], F32, name="b3")
+            b4 = work.tile([P, S], F32, name="b4")
+            for picked, offsets in ((b3, n3_l), (b4, n4_l)):
+                for u in range(2):
+                    nc.scalar.activation(
+                        picked[:, W * u : W * (u + 1)], b_rows[:].indirect(offsets[:, 16 * u : 16 * (u + 1)]), ACT.Copy
+                    )
+            upper = work.tile([P, S], F32, name="upper")
+            nc.vector.tensor_tensor(upper[:], b_rows[:], b3[:], ALU.max)
+            clipped = work.tile([P, S], F32, name="clipped")
+            nc.vector.tensor_tensor(clipped[:], upper[:], b4[:], ALU.min)
+            return clipped
+
+        w_words = keep.tile([P, 2, N], I32, name="w_words", align_bytes=64)
+        w_bytes = keep.tile([P, N], U8, name="w_bytes", align_bytes=64)
+        for j in range(2):
+            deal(w_words[:, j, :], w_table[:, j, :])
+        picked = [duel_pick(0)]
+        dt_rows = [duel_put(*picked[0])]
+        picked.append(duel_pick(1))
+        clipped = []
+        for t in range(PACK):
+            clipped.append(clip(t))
+            if t + 2 < PACK:
+                picked.append(duel_pick(t + 2))
+            if t + 1 < PACK:
+                dt_rows.append(duel_put(*picked[t + 1]))
+            if t == 0:
+                deal(w_bytes[:], w_bytes_raw[:])
+            if t >= 2:
+                round_rows(True, 1, t, clipped[t][:], gm_t)
+        for t in range(2):
+            round_rows(False, 0, t, dt_rows[t][:], gn_t)
+            round_rows(False, 1, t, clipped[t][:], gm_t)
+        for t in range(2, PACK):
+            round_rows(False, 0, t, dt_rows[t][:], gn_t)
+        quantize_rows(True, 1)
+        quantize_rows(False, 0)
+
+        h_banks = [psum.tile([P, S], F32, name="bank_h%d" % t, tag="bank_a%d" % t) for t in range(PACK)]
+        for j in (1, 0):
+            for t in range(PACK):
+                cols = slice(P * t, P * (t + 1))
+                nc.tensor.matmul_mx(
+                    h_banks[t][:], lhsT=w_words[:, j, cols].bitcast(FP8X4), lhsT_scale=w_bytes[4 * j :, cols],
+                    rhs=z_codes[j][:].bitcast(FP8X4), rhs_scale=z_bytes[j][:], start=(j == 1), stop=(j == 0),
+                )
+        for t in range(PACK):
+            if t == 1:
+                nc.scalar.copy(h_rows[t][:, :S], h_banks[t][:])
+            else:
+                nc.vector.tensor_copy(h_rows[t][:, :S], h_banks[t][:])
+
+        out_rows = out_0.rearrange("(p t) j -> p t j", t=PACK)
+        out_words = words_in_hbm(out_1)
+        out_bytes = keep.tile([P, S], U8, name="out_bytes", align_bytes=64)
+        def extremes_of(c, u, cols, smallest, largest):
+            width = cols.stop - cols.start
+            offsets = n5_l[:, cols.start * MEMBERS // 16 : cols.stop * MEMBERS // 16]
+            tag = "members_first%d" % (c % 2) if u == 0 else "members_second"
+            members = work.tile([P, 2, width * MEMBERS], F32, name="members", tag=tag, bufs=1)
+            for e in range(2):
+                nc.scalar.activation(members[:, e, :], h_rows[2 * u + e][:].indirect(offsets), ACT.Copy)
+            quads = members[:].rearrange("p e (j m) -> p (e j) m", m=MEMBERS)
+            steps = []
+            for op, name, extreme in ((ALU.min, "pair_min", smallest), (ALU.max, "pair_max", largest)):
+                pairs = work.tile([P, 2 * width, 2], F32, name=name)
+                nc.vector.tensor_tensor(pairs[:], quads[:, :, 0:2], quads[:, :, 2:4], op)
+                steps.append((op, pairs, extreme[:, 2 * u : 2 * u + 2, :].rearrange("p e j -> p (e j)")))
+            for op, pairs, extreme in steps:
+                nc.vector.tensor_tensor(extreme, pairs[:, :, 0], pairs[:, :, 1], op)
+
+        def subtract(u, cols, smallest, above):
+            for t in (2 * u, 2 * u + 1):
+                nc.vector.tensor_tensor(above[:, t, :], h_rows[t][:, cols], smallest[:, t, :], ALU.subtract)
+
+        def finish(cols, largest, above):
+            width = cols.stop - cols.start
+            bent = work.tile([P, PACK, width], F32, name="bent")
+            nc.scalar.activation(bent[:], above[:], ACT.Tanh)
+            result = work.tile([P, PACK, width], F32, name="result")
+            nc.vector.tensor_tensor(result[:], largest[:], bent[:], ALU.mult)
+            nc.sync.dma_start(out_rows[:, :, cols], result[:])
+            grouped = work.tile([P, width, PACK], BF16, name="grouped", align_bytes=64)
+            nc.vector.tensor_copy(grouped[:], result[:].rearrange("p t j -> p j t"))
+            codes = work.tile([P, width], I32, name="codes", align_bytes=64)
+            nc.vector.quantize_mx(codes[:].bitcast(FP8X4), out_bytes[:, cols], grouped[:].rearrange("p j t -> p (j t)"))
+            nc.sync.dma_start(out_words[:, cols], codes[:])
+
+        start = 0
+        waiting = None
+        for c, width in enumerate(CHUNKS):
+            cols = slice(start, start + width)
+            start = start + width
+            smallest = work.tile([P, PACK, width], F32, name="smallest")
+            largest = work.tile([P, PACK, width], F32, name="largest")
+            extremes_of(c, 0, cols, smallest, largest)
+            above = work.tile([P, PACK, width], F32, name="above", tag="members_first%d" % (c % 2), bufs=1)
+            subtract(0, cols, smallest, above)
+            if waiting is not None:
+                finish(*waiting)
+            extremes_of(c, 1, cols, smallest, largest)
+            subtract(1, cols, smallest, above)
+            waiting = (cols, largest, above)
+        finish(*waiting)
+        for q in range(4):
+            queue = nc.sync if q % 2 == 0 else nc.scalar
+            queue.dma_start(out_2[0, 4 * q : 4 * q + 4, :].bitcast(I32), out_bytes[32 * q : 32 * q + 4, :].bitcast(I32))

@@ -17,7 +17,7 @@ ACT = mybir.ActivationFunctionType
 
 P = 128
 PACK = 4
-CHUNKS = (128,128,128,128)
+CHUNK = 128
 SPARE = 16
 MEMBERS = 4
 
@@ -43,18 +43,18 @@ def tile_picked_kjduelminmxgtan_none_po_kernel(
             return tile
 
         def deal(out, in_):
-            nc.vector.tensor_copy(out.rearrange("p (t m) -> p t m", t=PACK), in_.rearrange("p (m t) -> p t m", t=PACK))
+            nc.vector.tensor_copy(out.rearrange("p (t m) -> p m t", t=PACK), in_.rearrange("p (m t) -> p m t", t=PACK))
 
         d_bytes = keep.tile([P, G], U8, name="d_bytes", align_bytes=64)
         x_bytes = keep.tile([P, T], U8, name="x_bytes", tag="bytes_in", align_bytes=64)
-        nc.gpsimd.memset(d_bytes[:].bitcast(I32), 0)
-        nc.gpsimd.memset(x_bytes[:].bitcast(I32), 0)
-        k1_l = load_list(k1, "k1_l")
-        offs_l = load_list(offs, "offs_l")
-        for e in range(2):
-            nc.sync.dma_start(d_bytes[e:P:16, :].bitcast(I32), d_scales[0, e:16:2, :].bitcast(I32))
+        nc.vector.memset(d_bytes[:].bitcast(I32), 0)
+        nc.vector.memset(x_bytes[:].bitcast(I32), 0)
         x_table = keep.tile([P, T], I32, name="x_table", align_bytes=64)
         nc.sync.dma_start(x_table[:], words_in_hbm(x_words))
+        k1_l = load_list(k1, "k1_l")
+        for e in range(2):
+            nc.sync.dma_start(d_bytes[e:P:16, :].bitcast(I32), d_scales[0, e:16:2, :].bitcast(I32))
+        offs_l = load_list(offs, "offs_l")
         d_table = keep.tile([P, G], I32, name="d_table", tag="words_in", align_bytes=64)
         nc.sync.dma_start(d_table[:], words_in_hbm(d_words))
         for q in range(4):
@@ -111,8 +111,8 @@ def tile_picked_kjduelminmxgtan_none_po_kernel(
         b_banks = scores(xb_words, xb_bytes, "bank_b")
 
         w_table = keep.tile([P, 2, N], I32, name="w_table", tag="words_in", align_bytes=64)
-        nc.sync.dma_start(w_table[:, 0, :], words_in_hbm(w1_words))
-        nc.sync.dma_start(w_table[:, 1, :], words_in_hbm(w2_words))
+        nc.scalar.dma_start(w_table[:, 0, :], words_in_hbm(w1_words))
+        nc.scalar.dma_start(w_table[:, 1, :], words_in_hbm(w2_words))
         w_bytes_raw = keep.tile([P, N], U8, name="w_bytes_raw", tag="bytes_in", align_bytes=64)
         nc.gpsimd.memset(w_bytes_raw[:].bitcast(I32), 0)
         for j, scales in enumerate((w1_scales, w2_scales)):
@@ -120,54 +120,58 @@ def tile_picked_kjduelminmxgtan_none_po_kernel(
                 rows = slice(32 * q + 4 * j, 32 * q + 4 * j + 4)
                 nc.sync.dma_start(w_bytes_raw[rows, :].bitcast(I32), scales[0, 4 * q : 4 * q + 4, :].bitcast(I32))
 
-        z_pairs = [keep.tile([P, 2, S, 2], BF16, name="z_pairs%d" % j, align_bytes=64) for j in range(2)]
-        z_codes = [keep.tile([P, S], U32, name="z_codes%d" % j, align_bytes=64) for j in range(2)]
-        z_bytes = [keep.tile([P, S], U8, name="z_bytes%d" % j, align_bytes=64) for j in range(2)]
+        half_gain = keep.tile([P, 2, PACK], F32, name="half_gain")
+        nc.scalar.activation(half_gain[:, 0, :], gn_t[:], ACT.Copy, scale=-0.5)
+        nc.scalar.activation(half_gain[:, 1, :], gn_t[:], ACT.Copy, scale=0.5)
+        z_pairs = keep.tile([P, 2, S, 2], BF16, name="z_pairs", align_bytes=64)
+        z2_pairs = keep.tile([P, 2, S, 2], BF16, name="z2_pairs", align_bytes=64)
 
-        def round_rows(on_vector, j, t, values, gain):
-            out = z_pairs[j][:, t // 2, :, t % 2]
-            if on_vector:
-                nc.vector.tensor_scalar(out, values, gain[:, t : t + 1], None, ALU.mult)
+        def round_z(t, cols=slice(0, S)):
+            nc.scalar.copy(z_pairs[:, t // 2, cols, t % 2], z_rows[t][:, cols])
+
+        def round_z2(t, cols=slice(0, S)):
+            out = z2_pairs[:, t // 2, cols, t % 2]
+            if True:
+                nc.vector.tensor_scalar(out, clipped[t][:, cols], gm_t[:, t : t + 1], None, ALU.mult)
             else:
-                nc.scalar.activation(out, values, ACT.Copy, scale=gain[:, t : t + 1])
+                nc.scalar.activation(out, clipped[t][:, cols], ACT.Copy, scale=gm_t[:, t : t + 1])
 
-        def quantize_rows(on_vector, j):
-            grouped = keep.tile([P, S, 2], U32, name="z_grouped%d" % j, align_bytes=64)
-            pairs = z_pairs[j][:].rearrange("p u s e -> p u (s e)")
-            if on_vector:
-                nc.vector.tensor_copy(grouped[:].bitcast(I32), pairs.bitcast(I32).rearrange("p u s -> p s u"))
-            else:
-                nc.scalar.copy(grouped[:], pairs.bitcast(U32).rearrange("p u s -> p s u"))
-            nc.vector.quantize_mx(
-                z_codes[j][:].bitcast(FP8X4), z_bytes[j][:], grouped[:].rearrange("p s u -> p (s u)").bitcast(BF16)
-            )
+        def pair_words(pairs, dtype, cols):
+            return pairs[:].rearrange("p u s e -> p u (s e)").bitcast(dtype)[:, :, cols].rearrange("p u s -> p s u")
 
-        def duel_pick(t):
-            a_rows = work.tile([P, S], F32, name="a_rows", bufs=4)
-            nc.scalar.activation(a_rows[:], a_banks[t][:], ACT.Copy, scale=0.0625)
+        def duel_pick(t, a_rows):
             pa = work.tile([P, W], F32, name="pa")
             pb = work.tile([P, W], F32, name="pb")
             nc.scalar.activation(pa[:], a_rows[:].indirect(n1_l[:]), ACT.Copy)
             nc.scalar.activation(pb[:], a_rows[:].indirect(n2_l[:]), ACT.Copy)
-            gap = work.tile([P, W], F32, name="gap")
+            gap = work.tile([P, W], F32, name="gap", tag="gap%d" % t, bufs=1)
             nc.vector.tensor_tensor(gap[:], pb[:], pa[:], ALU.subtract)
             return pa, pb, gap
 
-        def duel_put(pa, pb, gap):
-            half = work.tile([P, W], F32, name="half")
+        def a_out(t):
+            a_rows = work.tile([P, S], F32, name="a_rows", tag="a_first" if t < 2 else "gap%d" % (t - 2), bufs=1)
+            nc.scalar.activation(a_rows[:], a_banks[t][:], ACT.Copy, scale=0.0625)
+            return a_rows
+
+        def duel_put(t, pa, pb, gap):
+            half = work.tile([P, W], F32, name="half", tag="half%d" % t, bufs=1)
             nc.scalar.activation(half[:], gap[:], ACT.Tanh, scale=0.5)
             share_a = work.tile([P, W], F32, name="share_a")
             share_b = work.tile([P, W], F32, name="share_b")
-            nc.vector.tensor_scalar(share_a[:], half[:], -0.5, 0.5, ALU.mult, ALU.add)
-            nc.vector.tensor_scalar(share_b[:], half[:], 0.5, 0.5, ALU.mult, ALU.add)
-            dt_rows = work.tile([P, S], F32, name="dt_rows")
-            nc.vector.tensor_tensor(dt_rows[:].indirect(n1_l[:]), pa[:], share_a[:], ALU.mult)
-            nc.vector.tensor_tensor(dt_rows[:].indirect(n2_l[:]), pb[:], share_b[:], ALU.mult)
-            return dt_rows
+            down, up = half_gain[:, 0, t : t + 1], half_gain[:, 1, t : t + 1]
+            nc.vector.tensor_scalar(share_a[:], half[:], down, up, ALU.mult, ALU.add)
+            nc.vector.tensor_scalar(share_b[:], half[:], up, up, ALU.mult, ALU.add)
+            rows = work.tile([P, S], F32, name="z_rows")
+            nc.vector.tensor_tensor(rows[:].indirect(n1_l[:]), pa[:], share_a[:], ALU.mult)
+            nc.vector.tensor_tensor(rows[:].indirect(n2_l[:]), pb[:], share_b[:], ALU.mult)
+            return rows
 
-        def clip(t):
-            b_rows = work.tile([P, S], F32, name="b_rows", bufs=4)
+        def b_out(t):
+            b_rows = work.tile([P, S], F32, name="b_rows", tag="half%d" % t, bufs=1)
             nc.scalar.activation(b_rows[:], b_banks[t][:], ACT.Copy, scale=0.0625)
+            return b_rows
+
+        def clip(b_rows):
             b3 = work.tile([P, S], F32, name="b3")
             b4 = work.tile([P, S], F32, name="b4")
             for picked, offsets in ((b3, n3_l), (b4, n4_l)):
@@ -177,102 +181,132 @@ def tile_picked_kjduelminmxgtan_none_po_kernel(
                     )
             upper = work.tile([P, S], F32, name="upper")
             nc.vector.tensor_tensor(upper[:], b_rows[:], b3[:], ALU.max)
-            clipped = work.tile([P, S], F32, name="clipped")
-            nc.vector.tensor_tensor(clipped[:], upper[:], b4[:], ALU.min)
-            return clipped
+            lower = work.tile([P, S], F32, name="clipped")
+            nc.vector.tensor_tensor(lower[:], upper[:], b4[:], ALU.min)
+            return lower
 
         w_words = keep.tile([P, 2, N], I32, name="w_words", align_bytes=64)
         w_bytes = keep.tile([P, N], U8, name="w_bytes", align_bytes=64)
         for j in range(2):
             deal(w_words[:, j, :], w_table[:, j, :])
-        picked = [duel_pick(0)]
-        dt_rows = [duel_put(*picked[0])]
-        picked.append(duel_pick(1))
+        picked = duel_pick(0, a_out(0))
+        a_next = a_out(1)
+        z_rows = [duel_put(0, *picked)]
+        picked = duel_pick(1, a_next)
         clipped = []
         for t in range(PACK):
-            clipped.append(clip(t))
+            b_rows = b_out(t)
             if t + 2 < PACK:
-                picked.append(duel_pick(t + 2))
+                a_next = a_out(t + 2)
+            if t >= 2:
+                round_z(t - 2)
+            if 1 <= t:
+                round_z2(t - 1)
+            clipped.append(clip(b_rows))
             if t + 1 < PACK:
-                dt_rows.append(duel_put(*picked[t + 1]))
+                z_rows.append(duel_put(t + 1, *picked))
+            if t + 2 < PACK:
+                picked = duel_pick(t + 2, a_next)
             if t == 0:
                 deal(w_bytes[:], w_bytes_raw[:])
-            if t >= 2:
-                round_rows(True, 1, t, clipped[t][:], gm_t)
-        for t in range(2):
-            round_rows(False, 0, t, dt_rows[t][:], gn_t)
-            round_rows(False, 1, t, clipped[t][:], gm_t)
-        for t in range(2, PACK):
-            round_rows(False, 0, t, dt_rows[t][:], gn_t)
-        quantize_rows(True, 1)
-        quantize_rows(False, 0)
+        for t in range(PACK - 2, PACK):
+            round_z(t)
+        for t in range(PACK - 1, PACK - 1):
+            round_z2(t)
 
         h_banks = [psum.tile([P, S], F32, name="bank_h%d" % t, tag="bank_a%d" % t) for t in range(PACK)]
-        for j in (1, 0):
-            for t in range(PACK):
-                cols = slice(P * t, P * (t + 1))
+
+        def quantize(grouped, name):
+            codes = keep.tile([P, S], U32, name=name + "_codes", align_bytes=64)
+            scales = keep.tile([P, S], U8, name=name + "_bytes", align_bytes=64)
+            nc.vector.quantize_mx(codes[:].bitcast(FP8X4), scales[:], grouped[:].rearrange("p s u -> p (s u)").bitcast(BF16))
+            return codes, scales
+
+        z_grouped = keep.tile([P, S, 2], U32, name="z_grouped", tag="grouped_z", align_bytes=64)
+        nc.scalar.copy(z_grouped[:], pair_words(z_pairs, U32, slice(0, S)))
+        round_z2(PACK - 1)
+        operands = [quantize(z_grouped, "z")]
+        z2_grouped = keep.tile([P, S, 2], I32, name="z2_grouped", tag="grouped_z", align_bytes=64)
+        nc.vector.tensor_copy(z2_grouped[:], pair_words(z2_pairs, I32, slice(0, S)))
+        operands.append(quantize(z2_grouped, "z2"))
+        for t in range(PACK):
+            rows = slice(P * t, P * (t + 1))
+            for j, (codes, scales) in enumerate(operands):
                 nc.tensor.matmul_mx(
-                    h_banks[t][:], lhsT=w_words[:, j, cols].bitcast(FP8X4), lhsT_scale=w_bytes[4 * j :, cols],
-                    rhs=z_codes[j][:].bitcast(FP8X4), rhs_scale=z_bytes[j][:], start=(j == 1), stop=(j == 0),
+                    h_banks[t][:], lhsT=w_words[:, j, rows].bitcast(FP8X4), lhsT_scale=w_bytes[4 * j :, rows],
+                    rhs=codes[:].bitcast(FP8X4), rhs_scale=scales[:], start=(j == 0), stop=(j == 1),
                 )
         for t in range(PACK):
-            if t == 1:
-                nc.scalar.copy(h_rows[t][:, :S], h_banks[t][:])
-            else:
-                nc.vector.tensor_copy(h_rows[t][:, :S], h_banks[t][:])
+            nc.vector.tensor_copy(h_rows[t][:, :S], h_banks[t][:])
 
         out_rows = out_0.rearrange("(p t) j -> p t j", t=PACK)
         out_words = words_in_hbm(out_1)
         out_bytes = keep.tile([P, S], U8, name="out_bytes", align_bytes=64)
-        def extremes_of(c, u, cols, smallest, largest):
-            width = cols.stop - cols.start
+        def extreme_steps(c, u, largest):
+            cols = slice(CHUNK * c, CHUNK * (c + 1))
             offsets = n5_l[:, cols.start * MEMBERS // 16 : cols.stop * MEMBERS // 16]
-            tag = "members_first%d" % (c % 2) if u == 0 else "members_second"
-            members = work.tile([P, 2, width * MEMBERS], F32, name="members", tag=tag, bufs=1)
+            members = work.tile([P, 2, CHUNK * MEMBERS], F32, name="members", tag="members%d" % u, bufs=1)
             for e in range(2):
                 nc.scalar.activation(members[:, e, :], h_rows[2 * u + e][:].indirect(offsets), ACT.Copy)
             quads = members[:].rearrange("p e (j m) -> p (e j) m", m=MEMBERS)
-            steps = []
-            for op, name, extreme in ((ALU.min, "pair_min", smallest), (ALU.max, "pair_max", largest)):
-                pairs = work.tile([P, 2 * width, 2], F32, name=name)
-                nc.vector.tensor_tensor(pairs[:], quads[:, :, 0:2], quads[:, :, 2:4], op)
-                steps.append((op, pairs, extreme[:, 2 * u : 2 * u + 2, :].rearrange("p e j -> p (e j)")))
-            for op, pairs, extreme in steps:
-                nc.vector.tensor_tensor(extreme, pairs[:, :, 0], pairs[:, :, 1], op)
+            pair_min = work.tile([P, 2 * CHUNK, 2], F32, name="pair_min")
+            pair_max = work.tile([P, 2 * CHUNK, 2], F32, name="pair_max")
+            smallest = work.tile([P, 2, CHUNK], F32, name="smallest")
+            above = work.tile([P, 2, CHUNK], F32, name="above", tag=("above", "members1")[u], bufs=(2, 1)[u])
+            flat = "p e j -> p (e j)"
+            steps = [
+                lambda: nc.vector.tensor_tensor(pair_min[:], quads[:, :, 0:2], quads[:, :, 2:4], ALU.min),
+                lambda: nc.vector.tensor_tensor(pair_max[:], quads[:, :, 0:2], quads[:, :, 2:4], ALU.max),
+                lambda: nc.vector.tensor_tensor(smallest[:].rearrange(flat), pair_min[:, :, 0], pair_min[:, :, 1], ALU.min),
+                lambda: nc.vector.tensor_tensor(
+                    largest[:, 2 * u : 2 * u + 2, :].rearrange(flat), pair_max[:, :, 0], pair_max[:, :, 1], ALU.max
+                ),
+                lambda: nc.vector.tensor_tensor(above[:, 0, :], h_rows[2 * u][:, cols], smallest[:, 0, :], ALU.subtract),
+                lambda: nc.vector.tensor_tensor(above[:, 1, :], h_rows[2 * u + 1][:, cols], smallest[:, 1, :], ALU.subtract),
+            ]
+            return steps, above
 
-        def subtract(u, cols, smallest, above):
-            for t in (2 * u, 2 * u + 1):
-                nc.vector.tensor_tensor(above[:, t, :], h_rows[t][:, cols], smallest[:, t, :], ALU.subtract)
+        def finish_steps(c, largest, above, groups):
+            cols = slice(CHUNK * c, CHUNK * (c + 1))
+            bent = work.tile([P, PACK, CHUNK], F32, name="bent")
+            result = work.tile([P, PACK, CHUNK], F32, name="result")
+            grouped = work.tile([P, CHUNK, PACK], BF16, name="grouped", align_bytes=64)
+            codes = work.tile([P, CHUNK], I32, name="codes", align_bytes=64)
 
-        def finish(cols, largest, above):
-            width = cols.stop - cols.start
-            bent = work.tile([P, PACK, width], F32, name="bent")
-            nc.scalar.activation(bent[:], above[:], ACT.Tanh)
-            result = work.tile([P, PACK, width], F32, name="result")
-            nc.vector.tensor_tensor(result[:], largest[:], bent[:], ALU.mult)
-            nc.sync.dma_start(out_rows[:, :, cols], result[:])
-            grouped = work.tile([P, width, PACK], BF16, name="grouped", align_bytes=64)
-            nc.vector.tensor_copy(grouped[:], result[:].rearrange("p t j -> p j t"))
-            codes = work.tile([P, width], I32, name="codes", align_bytes=64)
-            nc.vector.quantize_mx(codes[:].bitcast(FP8X4), out_bytes[:, cols], grouped[:].rearrange("p j t -> p (j t)"))
-            nc.sync.dma_start(out_words[:, cols], codes[:])
+            def multiply():
+                for u in range(2):
+                    nc.scalar.activation(bent[:, 2 * u : 2 * u + 2, :], above[u][:], ACT.Tanh)
+                for tiles in groups:
+                    nc.vector.tensor_tensor(result[:, tiles, :], largest[:, tiles, :], bent[:, tiles, :], ALU.mult)
+                nc.sync.dma_start(out_rows[:, :, cols], result[:])
 
-        start = 0
-        waiting = None
-        for c, width in enumerate(CHUNKS):
-            cols = slice(start, start + width)
-            start = start + width
-            smallest = work.tile([P, PACK, width], F32, name="smallest")
-            largest = work.tile([P, PACK, width], F32, name="largest")
-            extremes_of(c, 0, cols, smallest, largest)
-            above = work.tile([P, PACK, width], F32, name="above", tag="members_first%d" % (c % 2), bufs=1)
-            subtract(0, cols, smallest, above)
-            if waiting is not None:
-                finish(*waiting)
-            extremes_of(c, 1, cols, smallest, largest)
-            subtract(1, cols, smallest, above)
-            waiting = (cols, largest, above)
-        finish(*waiting)
+            def regroup():
+                nc.vector.tensor_copy(
+                    grouped[:].rearrange("p (c i) t -> p c t i", i=4), result[:].rearrange("p t (c i) -> p c t i", i=4)
+                )
+
+            def quantize_out():
+                nc.vector.quantize_mx(codes[:].bitcast(FP8X4), out_bytes[:, cols], grouped[:].rearrange("p j t -> p (j t)"))
+                nc.sync.dma_start(out_words[:, cols], codes[:])
+
+            return [multiply, regroup, quantize_out]
+
+        pending = []
+        for c in range(S // CHUNK):
+            largest = work.tile([P, PACK, CHUNK], F32, name="largest")
+            steps, above_first = extreme_steps(c, 0, largest)
+            for place, step in enumerate(steps):
+                step()
+                if pending and place >= 1:
+                    pending.pop(0)()
+            steps, above_second = extreme_steps(c, 1, largest)
+            for step in steps:
+                step()
+            last = c + 1 == S // CHUNK
+            groups = [slice(0, 2), slice(2, 4)] if last else [slice(0, PACK)]
+            pending = finish_steps(c, largest, (above_first, above_second), groups)
+        for step in pending:
+            step()
         for q in range(4):
             queue = nc.sync if q % 2 == 0 else nc.scalar
             queue.dma_start(out_2[0, 4 * q : 4 * q + 4, :].bitcast(I32), out_bytes[32 * q : 32 * q + 4, :].bitcast(I32))

@@ -127,11 +127,11 @@ def tile_picked_kjduelminmxgtan_none_po_kernel(
         z2_pairs = keep.tile([P, 2, S, 2], BF16, name="z2_pairs", align_bytes=64)
 
         def round_z(t, cols=slice(0, S)):
-            nc.scalar.copy(z_pairs[:, t // 2, cols, t % 2], z_rows[t][:, cols])
+            (nc.vector.tensor_copy if False else nc.scalar.copy)(z_pairs[:, t // 2, cols, t % 2], z_rows[t][:, cols])
 
         def round_z2(t, cols=slice(0, S)):
             out = z2_pairs[:, t // 2, cols, t % 2]
-            if True:
+            if t >= 2:
                 nc.vector.tensor_scalar(out, clipped[t][:, cols], gm_t[:, t : t + 1], None, ALU.mult)
             else:
                 nc.scalar.activation(out, clipped[t][:, cols], ACT.Copy, scale=gm_t[:, t : t + 1])
@@ -149,7 +149,7 @@ def tile_picked_kjduelminmxgtan_none_po_kernel(
             return pa, pb, gap
 
         def a_out(t):
-            a_rows = work.tile([P, S], F32, name="a_rows", tag="a_first" if t < 2 else "gap%d" % (t - 2), bufs=1)
+            a_rows = work.tile([P, S], F32, name="a_rows", tag="gap0" if t == 2 else "a_first", bufs=1)
             nc.scalar.activation(a_rows[:], a_banks[t][:], ACT.Copy, scale=0.0625)
             return a_rows
 
@@ -167,7 +167,7 @@ def tile_picked_kjduelminmxgtan_none_po_kernel(
             return rows
 
         def b_out(t):
-            b_rows = work.tile([P, S], F32, name="b_rows", tag="half%d" % t, bufs=1)
+            b_rows = work.tile([P, S], F32, name="b_rows", tag="gap%d" % (t + 1) if t < 3 else "gap0", bufs=1)
             nc.scalar.activation(b_rows[:], b_banks[t][:], ACT.Copy, scale=0.0625)
             return b_rows
 
@@ -189,55 +189,64 @@ def tile_picked_kjduelminmxgtan_none_po_kernel(
         w_bytes = keep.tile([P, N], U8, name="w_bytes", align_bytes=64)
         for j in range(2):
             deal(w_words[:, j, :], w_table[:, j, :])
-        picked = duel_pick(0, a_out(0))
-        a_next = a_out(1)
-        z_rows = [duel_put(0, *picked)]
-        picked = duel_pick(1, a_next)
+        picked = [duel_pick(0, a_out(0))]
+        a_rows = a_out(1)
+        z_rows = [duel_put(0, *picked[0])]
+        picked.append(duel_pick(1, a_rows))
+        a_next = a_out(2)
+        a_rows = a_out(3)
+        picked.append(duel_pick(2, a_next))
+        z_rows.append(duel_put(1, *picked[1]))
+        picked.append(duel_pick(3, a_rows))
+        deal(w_bytes[:], w_bytes_raw[:])
         clipped = []
         for t in range(PACK):
             b_rows = b_out(t)
             if t + 2 < PACK:
-                a_next = a_out(t + 2)
-            if t >= 2:
-                round_z(t - 2)
-            if 1 <= t:
-                round_z2(t - 1)
+                z_rows.append(duel_put(t + 2, *picked[t + 2]))
             clipped.append(clip(b_rows))
-            if t + 1 < PACK:
-                z_rows.append(duel_put(t + 1, *picked))
-            if t + 2 < PACK:
-                picked = duel_pick(t + 2, a_next)
-            if t == 0:
-                deal(w_bytes[:], w_bytes_raw[:])
-        for t in range(PACK - 2, PACK):
+
+        for t in range(PACK - 1):
             round_z(t)
-        for t in range(PACK - 1, PACK - 1):
-            round_z2(t)
 
-        h_banks = [psum.tile([P, S], F32, name="bank_h%d" % t, tag="bank_a%d" % t) for t in range(PACK)]
+        codes = [keep.tile([P, S], U32, name="z_codes%d" % j, align_bytes=64) for j in range(2)]
+        scales = [keep.tile([P, S], U8, name="z_bytes%d" % j, align_bytes=64) for j in range(2)]
 
-        def quantize(grouped, name):
-            codes = keep.tile([P, S], U32, name=name + "_codes", align_bytes=64)
-            scales = keep.tile([P, S], U8, name=name + "_bytes", align_bytes=64)
-            nc.vector.quantize_mx(codes[:].bitcast(FP8X4), scales[:], grouped[:].rearrange("p s u -> p (s u)").bitcast(BF16))
-            return codes, scales
+        def quantize(j, grouped, cols):
+            values = grouped[:, cols, :].rearrange("p s u -> p (s u)").bitcast(BF16)
+            nc.vector.quantize_mx(codes[j][:, cols].bitcast(FP8X4), scales[j][:, cols], values)
 
-        z_grouped = keep.tile([P, S, 2], U32, name="z_grouped", tag="grouped_z", align_bytes=64)
-        nc.scalar.copy(z_grouped[:], pair_words(z_pairs, U32, slice(0, S)))
-        round_z2(PACK - 1)
-        operands = [quantize(z_grouped, "z")]
-        z2_grouped = keep.tile([P, S, 2], I32, name="z2_grouped", tag="grouped_z", align_bytes=64)
-        nc.vector.tensor_copy(z2_grouped[:], pair_words(z2_pairs, I32, slice(0, S)))
-        operands.append(quantize(z2_grouped, "z2"))
-        for t in range(PACK):
+        def h_pass(j, t, cols, out):
             rows = slice(P * t, P * (t + 1))
-            for j, (codes, scales) in enumerate(operands):
-                nc.tensor.matmul_mx(
-                    h_banks[t][:], lhsT=w_words[:, j, rows].bitcast(FP8X4), lhsT_scale=w_bytes[4 * j :, rows],
-                    rhs=codes[:].bitcast(FP8X4), rhs_scale=scales[:], start=(j == 0), stop=(j == 1),
-                )
+            nc.tensor.matmul_mx(
+                out, lhsT=w_words[:, j, rows].bitcast(FP8X4), lhsT_scale=w_bytes[4 * j :, rows],
+                rhs=codes[j][:, cols].bitcast(FP8X4), rhs_scale=scales[j][:, cols], start=(j == 0), stop=(j == 1),
+            )
+
+        whole = slice(0, S)
+        halves = [slice(0, S // 2), slice(S // 2, S)]
+        z_grouped = keep.tile([P, S, 2], I32, name="z_grouped", align_bytes=64)
+        z2_grouped = keep.tile([P, S, 2], I32, name="z2_grouped", align_bytes=64)
+        round_z(PACK - 1)
+        nc.vector.tensor_copy(z_grouped[:], pair_words(z_pairs, I32, whole))
         for t in range(PACK):
-            nc.vector.tensor_copy(h_rows[t][:, :S], h_banks[t][:])
+            round_z2(t)
+        quantize(0, z_grouped, whole)
+        for cols in halves:
+            nc.vector.tensor_copy(z2_grouped[:, cols, :], pair_words(z2_pairs, I32, cols))
+        for cols in halves:
+            quantize(1, z2_grouped, cols)
+        first_banks = [psum.tile([P, S // 2], F32, name="bank_h0_%d" % u, tag=("bank_a0", "bank_b0")[u]) for u in range(2)]
+        for j in range(2):
+            for u, cols in enumerate(halves):
+                h_pass(j, 0, cols, first_banks[u][:])
+        nc.scalar.copy(h_rows[0][:, halves[0]], first_banks[0][:])
+        nc.vector.tensor_copy(h_rows[0][:, halves[1]], first_banks[1][:])
+        for t in range(1, PACK):
+            bank = psum.tile([P, S], F32, name="bank_h%d" % t, tag=("bank_a1", "bank_a0", "bank_b0")[t - 1])
+            for j in range(2):
+                h_pass(j, t, whole, bank[:])
+            nc.vector.tensor_copy(h_rows[t][:, :S], bank[:])
 
         out_rows = out_0.rearrange("(p t) j -> p t j", t=PACK)
         out_words = words_in_hbm(out_1)

@@ -2,7 +2,7 @@ from contextlib import ExitStack
 
 import concourse.mybir as mybir
 
-K, T, S, N, G, H, W = 512, 1024, 512, 512, 2048, 512, 256
+T, S, N, G, H, W = 1024, 512, 512, 2048, 512, 256
 FLOPS = 4 * 2 * 512 * 512 * 512
 
 F32 = mybir.dt.float32
@@ -17,9 +17,12 @@ ACT = mybir.ActivationFunctionType
 
 P = 128
 PACK = 4
+QUADS = 4
+PER_COLUMN = 16
+MEMBERS = 4
 CHUNK = 128
 SPARE = 16
-MEMBERS = 4
+SCORE_SCALE = 0.0625
 
 
 def tile_picked_kjduelminmxgtan_none_po_kernel(
@@ -34,7 +37,7 @@ def tile_picked_kjduelminmxgtan_none_po_kernel(
     with ExitStack() as ctx:
         lists = ctx.enter_context(tc.tile_pool(name="lists", bufs=1))
         keep = ctx.enter_context(tc.tile_pool(name="keep", bufs=1))
-        work = ctx.enter_context(tc.tile_pool(name="work", bufs=4))
+        work = ctx.enter_context(tc.tile_pool(name="work", bufs=PACK))
         psum = ctx.enter_context(tc.psum_pool(name="psum", bufs=1))
 
         def load_list(source, name):
@@ -49,273 +52,273 @@ def tile_picked_kjduelminmxgtan_none_po_kernel(
         x_bytes = keep.tile([P, T], U8, name="x_bytes", tag="bytes_in", align_bytes=64)
         nc.vector.memset(d_bytes[:].bitcast(I32), 0)
         nc.vector.memset(x_bytes[:].bitcast(I32), 0)
-        x_table = keep.tile([P, T], I32, name="x_table", align_bytes=64)
-        nc.sync.dma_start(x_table[:], words_in_hbm(x_words))
-        k1_l = load_list(k1, "k1_l")
+        k1_list = load_list(k1, "k1_list")
+        offs_list = load_list(offs, "offs_list")
         for e in range(2):
             nc.sync.dma_start(d_bytes[e:P:16, :].bitcast(I32), d_scales[0, e:16:2, :].bitcast(I32))
-        offs_l = load_list(offs, "offs_l")
+        x_table = keep.tile([P, T], I32, name="x_table", align_bytes=64)
+        nc.sync.dma_start(x_table[:], words_in_hbm(x_words))
         d_table = keep.tile([P, G], I32, name="d_table", tag="words_in", align_bytes=64)
         nc.sync.dma_start(d_table[:], words_in_hbm(d_words))
-        for q in range(4):
+        for q in range(QUADS):
             nc.sync.dma_start(x_bytes[32 * q : 32 * q + 4, :].bitcast(I32), x_scales[0, 4 * q : 4 * q + 4, :].bitcast(I32))
-        two_l = load_list(two, "two_l")
-        n1_l = load_list(n1, "n1_l")
-        n2_l = load_list(n2, "n2_l")
-        n3_l = load_list(n3, "n3_l")
-        n4_l = load_list(n4, "n4_l")
-        n5_l = load_list(n5, "n5_l")
-        gn_t = keep.tile([P, PACK], F32, name="gn_t")
-        gm_t = keep.tile([P, PACK], F32, name="gm_t")
-        nc.gpsimd.dma_start(gn_t[:], gn.rearrange("(p t) o -> p (t o)", t=PACK))
-        nc.gpsimd.dma_start(gm_t[:], gm.rearrange("(p t) o -> p (t o)", t=PACK))
+        two_list = load_list(two, "two_list")
+        n1_list = load_list(n1, "n1_list")
+        n2_list = load_list(n2, "n2_list")
+        n3_list = load_list(n3, "n3_list")
+        n4_list = load_list(n4, "n4_list")
+        n5_list = load_list(n5, "n5_list")
+        gn_rows = keep.tile([P, PACK], F32, name="gn_rows")
+        gm_rows = keep.tile([P, PACK], F32, name="gm_rows")
+        nc.gpsimd.dma_start(gn_rows[:], gn.rearrange("(p t) o -> p (t o)", t=PACK))
+        nc.gpsimd.dma_start(gm_rows[:], gm.rearrange("(p t) o -> p (t o)", t=PACK))
 
         h_rows = [keep.tile([P, S + SPARE], F32, name="h_rows%d" % t) for t in range(PACK)]
         for t in range(PACK):
             nc.gpsimd.memset(h_rows[t][:, S:], 0.0)
 
-        key_bytes_raw = keep.tile([P, H], U8, name="key_bytes_raw", align_bytes=64)
+        picked_key_bytes = keep.tile([P, H], U8, name="picked_key_bytes", align_bytes=64)
         key_bytes = keep.tile([P, H], U8, name="key_bytes", align_bytes=64)
-        nc.vector.tensor_copy(key_bytes_raw[:], d_bytes[:].indirect(k1_l[:]))
-        deal(key_bytes[:], key_bytes_raw[:])
+        nc.vector.tensor_copy(picked_key_bytes[:], d_bytes[:].indirect(k1_list[:]))
+        deal(key_bytes[:], picked_key_bytes[:])
         for e in range(2):
             nc.scalar.dma_start(key_bytes[2 + e : P : 32, :].bitcast(I32), key_bytes[16 + e : P : 32, :].bitcast(I32))
 
         def pick_tokens(offsets, name):
             words = keep.tile([P, S], U32, name=name + "_words", align_bytes=64)
-            scales = keep.tile([P, S], U8, name=name + "_bytes", align_bytes=64)
+            scale_bytes = keep.tile([P, S], U8, name=name + "_bytes", align_bytes=64)
             nc.vector.tensor_copy(words[:], x_table[:].bitcast(U32).indirect(offsets[:]))
-            nc.vector.tensor_copy(scales[:], x_bytes[:].indirect(offsets[:]))
-            return words, scales
+            nc.vector.tensor_copy(scale_bytes[:], x_bytes[:].indirect(offsets[:]))
+            return words, scale_bytes
 
-        xa_words, xa_bytes = pick_tokens(offs_l, "xa")
-        key_words_raw = keep.tile([P, H], U32, name="key_words_raw", align_bytes=64)
+        a_tokens = pick_tokens(offs_list, "a_token")
+        picked_key_words = keep.tile([P, H], U32, name="picked_key_words", align_bytes=64)
         key_words = keep.tile([P, H], U32, name="key_words", align_bytes=64)
-        nc.vector.tensor_copy(key_words_raw[:], d_table[:].bitcast(U32).indirect(k1_l[:]))
-        deal(key_words[:], key_words_raw[:])
+        nc.vector.tensor_copy(picked_key_words[:], d_table[:].bitcast(U32).indirect(k1_list[:]))
+        deal(key_words[:], picked_key_words[:])
 
-        def scores(words, scales, name):
+        def score(words, scale_bytes, name):
             banks = []
             for t in range(PACK):
                 bank = psum.tile([P, S], F32, name="%s%d" % (name, t))
-                cols = slice(P * t, P * (t + 1))
+                keys = slice(P * t, P * (t + 1))
                 nc.tensor.matmul_mx(
-                    bank[:], lhsT=key_words[:, cols].bitcast(FP8X4), lhsT_scale=key_bytes[:, cols],
-                    rhs=words[:].bitcast(FP8X4), rhs_scale=scales[:], start=True, stop=True,
+                    bank[:], lhsT=key_words[:, keys].bitcast(FP8X4), lhsT_scale=key_bytes[:, keys],
+                    rhs=words[:].bitcast(FP8X4), rhs_scale=scale_bytes[:], start=True, stop=True,
                 )
                 banks.append(bank)
             return banks
 
-        a_banks = scores(xa_words, xa_bytes, "bank_a")
-        xb_words, xb_bytes = pick_tokens(two_l, "xb")
-        b_banks = scores(xb_words, xb_bytes, "bank_b")
+        a_banks = score(*a_tokens, "bank_a")
+        b_banks = score(*pick_tokens(two_list, "b_token"), "bank_b")
 
         w_table = keep.tile([P, 2, N], I32, name="w_table", tag="words_in", align_bytes=64)
         nc.scalar.dma_start(w_table[:, 0, :], words_in_hbm(w1_words))
         nc.scalar.dma_start(w_table[:, 1, :], words_in_hbm(w2_words))
-        w_bytes_raw = keep.tile([P, N], U8, name="w_bytes_raw", tag="bytes_in", align_bytes=64)
-        nc.gpsimd.memset(w_bytes_raw[:].bitcast(I32), 0)
-        for j, scales in enumerate((w1_scales, w2_scales)):
-            for q in range(4):
+        loaded_w_bytes = keep.tile([P, N], U8, name="loaded_w_bytes", tag="bytes_in", align_bytes=64)
+        nc.gpsimd.memset(loaded_w_bytes[:].bitcast(I32), 0)
+        for j, w_scales in enumerate((w1_scales, w2_scales)):
+            for q in range(QUADS):
                 rows = slice(32 * q + 4 * j, 32 * q + 4 * j + 4)
-                nc.sync.dma_start(w_bytes_raw[rows, :].bitcast(I32), scales[0, 4 * q : 4 * q + 4, :].bitcast(I32))
+                nc.sync.dma_start(loaded_w_bytes[rows, :].bitcast(I32), w_scales[0, 4 * q : 4 * q + 4, :].bitcast(I32))
 
-        half_gain = keep.tile([P, 2, PACK], F32, name="half_gain")
-        nc.scalar.activation(half_gain[:, 0, :], gn_t[:], ACT.Copy, scale=-0.5)
-        nc.scalar.activation(half_gain[:, 1, :], gn_t[:], ACT.Copy, scale=0.5)
-        z_pairs = keep.tile([P, 2, S, 2], BF16, name="z_pairs", align_bytes=64)
-        z2_pairs = keep.tile([P, 2, S, 2], BF16, name="z2_pairs", align_bytes=64)
+        half_gn = keep.tile([P, 2, PACK], F32, name="half_gn")
+        nc.scalar.activation(half_gn[:, 0, :], gn_rows[:], ACT.Copy, scale=-0.5)
+        nc.scalar.activation(half_gn[:, 1, :], gn_rows[:], ACT.Copy, scale=0.5)
 
-        def round_z(t, cols=slice(0, S)):
-            (nc.vector.tensor_copy if False else nc.scalar.copy)(z_pairs[:, t // 2, cols, t % 2], z_rows[t][:, cols])
+        a_tags = ("a_rows", "a_rows", "gap0", "a_rows")
+        b_tags = ("gap1", "gap2", "gap3", "gap0")
 
-        def round_z2(t, cols=slice(0, S)):
-            out = z2_pairs[:, t // 2, cols, t % 2]
-            if t >= 2:
-                nc.vector.tensor_scalar(out, clipped[t][:, cols], gm_t[:, t : t + 1], None, ALU.mult)
-            else:
-                nc.scalar.activation(out, clipped[t][:, cols], ACT.Copy, scale=gm_t[:, t : t + 1])
+        def empty_bank(bank, tag):
+            rows = work.tile([P, S], F32, name="score_rows", tag=tag, bufs=1)
+            nc.scalar.activation(rows[:], bank[:], ACT.Copy, scale=SCORE_SCALE)
+            return rows
 
-        def pair_words(pairs, dtype, cols):
-            return pairs[:].rearrange("p u s e -> p u (s e)").bitcast(dtype)[:, :, cols].rearrange("p u s -> p s u")
-
-        def duel_pick(t, a_rows):
+        def pick_pairs(t, a_rows):
             pa = work.tile([P, W], F32, name="pa")
             pb = work.tile([P, W], F32, name="pb")
-            nc.scalar.activation(pa[:], a_rows[:].indirect(n1_l[:]), ACT.Copy)
-            nc.scalar.activation(pb[:], a_rows[:].indirect(n2_l[:]), ACT.Copy)
+            nc.scalar.activation(pa[:], a_rows[:].indirect(n1_list[:]), ACT.Copy)
+            nc.scalar.activation(pb[:], a_rows[:].indirect(n2_list[:]), ACT.Copy)
             gap = work.tile([P, W], F32, name="gap", tag="gap%d" % t, bufs=1)
             nc.vector.tensor_tensor(gap[:], pb[:], pa[:], ALU.subtract)
             return pa, pb, gap
 
-        def a_out(t):
-            a_rows = work.tile([P, S], F32, name="a_rows", tag="gap0" if t == 2 else "a_first", bufs=1)
-            nc.scalar.activation(a_rows[:], a_banks[t][:], ACT.Copy, scale=0.0625)
-            return a_rows
-
-        def duel_put(t, pa, pb, gap):
-            half = work.tile([P, W], F32, name="half", tag="half%d" % t, bufs=1)
-            nc.scalar.activation(half[:], gap[:], ACT.Tanh, scale=0.5)
-            share_a = work.tile([P, W], F32, name="share_a")
-            share_b = work.tile([P, W], F32, name="share_b")
-            down, up = half_gain[:, 0, t : t + 1], half_gain[:, 1, t : t + 1]
-            nc.vector.tensor_scalar(share_a[:], half[:], down, up, ALU.mult, ALU.add)
-            nc.vector.tensor_scalar(share_b[:], half[:], up, up, ALU.mult, ALU.add)
+        def put_pairs(t, pa, pb, gap):
+            tanh_gap = work.tile([P, W], F32, name="tanh_gap")
+            nc.scalar.activation(tanh_gap[:], gap[:], ACT.Tanh, scale=0.5)
+            factor_a = work.tile([P, W], F32, name="factor_a")
+            factor_b = work.tile([P, W], F32, name="factor_b")
+            minus, plus = half_gn[:, 0, t : t + 1], half_gn[:, 1, t : t + 1]
+            nc.vector.tensor_scalar(factor_a[:], tanh_gap[:], minus, plus, ALU.mult, ALU.add)
+            nc.vector.tensor_scalar(factor_b[:], tanh_gap[:], plus, plus, ALU.mult, ALU.add)
             rows = work.tile([P, S], F32, name="z_rows")
-            nc.vector.tensor_tensor(rows[:].indirect(n1_l[:]), pa[:], share_a[:], ALU.mult)
-            nc.vector.tensor_tensor(rows[:].indirect(n2_l[:]), pb[:], share_b[:], ALU.mult)
+            nc.vector.tensor_tensor(rows[:].indirect(n1_list[:]), pa[:], factor_a[:], ALU.mult)
+            nc.vector.tensor_tensor(rows[:].indirect(n2_list[:]), pb[:], factor_b[:], ALU.mult)
             return rows
 
-        def b_out(t):
-            b_rows = work.tile([P, S], F32, name="b_rows", tag="gap%d" % (t + 1) if t < 3 else "gap0", bufs=1)
-            nc.scalar.activation(b_rows[:], b_banks[t][:], ACT.Copy, scale=0.0625)
-            return b_rows
-
-        def clip(b_rows):
-            b3 = work.tile([P, S], F32, name="b3")
-            b4 = work.tile([P, S], F32, name="b4")
-            for picked, offsets in ((b3, n3_l), (b4, n4_l)):
+        def larger_of(t, b_rows):
+            at_n3 = work.tile([P, S], F32, name="at_n3", tag="at_n3_%d" % t, bufs=1)
+            at_n4 = work.tile([P, S], F32, name="at_n4")
+            for picked, offsets in ((at_n3, n3_list), (at_n4, n4_list)):
                 for u in range(2):
-                    nc.scalar.activation(
-                        picked[:, W * u : W * (u + 1)], b_rows[:].indirect(offsets[:, 16 * u : 16 * (u + 1)]), ACT.Copy
-                    )
-            upper = work.tile([P, S], F32, name="upper")
-            nc.vector.tensor_tensor(upper[:], b_rows[:], b3[:], ALU.max)
-            lower = work.tile([P, S], F32, name="clipped")
-            nc.vector.tensor_tensor(lower[:], upper[:], b4[:], ALU.min)
-            return lower
+                    half_list = offsets[:, W // PER_COLUMN * u : W // PER_COLUMN * (u + 1)]
+                    nc.scalar.activation(picked[:, W * u : W * (u + 1)], b_rows[:].indirect(half_list), ACT.Copy)
+            larger = work.tile([P, S], F32, name="larger")
+            nc.vector.tensor_tensor(larger[:], b_rows[:], at_n3[:], ALU.max)
+            return larger, at_n4
+
+        def smaller_of(larger, at_n4, tag):
+            smaller = work.tile([P, S], F32, name="smaller", tag=tag, bufs=1)
+            nc.vector.tensor_tensor(smaller[:], larger[:], at_n4[:], ALU.min)
+            return smaller
 
         w_words = keep.tile([P, 2, N], I32, name="w_words", align_bytes=64)
         w_bytes = keep.tile([P, N], U8, name="w_bytes", align_bytes=64)
         for j in range(2):
             deal(w_words[:, j, :], w_table[:, j, :])
-        picked = [duel_pick(0, a_out(0))]
-        a_rows = a_out(1)
-        z_rows = [duel_put(0, *picked[0])]
-        picked.append(duel_pick(1, a_rows))
-        a_next = a_out(2)
-        a_rows = a_out(3)
-        picked.append(duel_pick(2, a_next))
-        z_rows.append(duel_put(1, *picked[1]))
-        picked.append(duel_pick(3, a_rows))
-        deal(w_bytes[:], w_bytes_raw[:])
-        clipped = []
+
+        pairs = [pick_pairs(0, empty_bank(a_banks[0], a_tags[0]))]
+        a_rows_1 = empty_bank(a_banks[1], a_tags[1])
+        z_rows = [put_pairs(0, *pairs[0])]
+        pairs.append(pick_pairs(1, a_rows_1))
+        a_rows_2 = empty_bank(a_banks[2], a_tags[2])
+        a_rows_3 = empty_bank(a_banks[3], a_tags[3])
+        pairs.append(pick_pairs(2, a_rows_2))
+        z_rows.append(put_pairs(1, *pairs[1]))
+        pairs.append(pick_pairs(3, a_rows_3))
+        deal(w_bytes[:], loaded_w_bytes[:])
+        compared, z2_rows = [], []
         for t in range(PACK):
-            b_rows = b_out(t)
+            b_rows = empty_bank(b_banks[t], b_tags[t])
             if t + 2 < PACK:
-                z_rows.append(duel_put(t + 2, *picked[t + 2]))
-            clipped.append(clip(b_rows))
+                z_rows.append(put_pairs(t + 2, *pairs[t + 2]))
+            compared.append(larger_of(t, b_rows))
+            if t + 2 < PACK:
+                z2_rows.append(smaller_of(*compared[t], "smaller%d" % t))
+        z2_rows.append(smaller_of(*compared[2], "at_n3_3"))
+        z2_rows.append(smaller_of(*compared[3], "smaller3"))
 
-        for t in range(PACK - 1):
-            round_z(t)
+        z_pairs = keep.tile([P, 2, S, 2], BF16, name="z_pairs", align_bytes=64)
+        z2_pairs = keep.tile([P, 2, S, 2], BF16, name="z2_pairs", align_bytes=64)
+        z_grouped = keep.tile([P, S, 2], I32, name="z_grouped", align_bytes=64)
+        z2_grouped = keep.tile([P, S, 2], I32, name="z2_grouped", align_bytes=64)
+        z_codes = [keep.tile([P, S], U32, name="z_codes%d" % j, align_bytes=64) for j in range(2)]
+        z_bytes = [keep.tile([P, S], U8, name="z_bytes%d" % j, align_bytes=64) for j in range(2)]
 
-        codes = [keep.tile([P, S], U32, name="z_codes%d" % j, align_bytes=64) for j in range(2)]
-        scales = [keep.tile([P, S], U8, name="z_bytes%d" % j, align_bytes=64) for j in range(2)]
+        def group(grouped, rounded, cols):
+            words = rounded[:].rearrange("p u s e -> p u (s e)").bitcast(I32)
+            nc.vector.tensor_copy(grouped[:, cols, :], words[:, :, cols].rearrange("p u s -> p s u"))
 
         def quantize(j, grouped, cols):
             values = grouped[:, cols, :].rearrange("p s u -> p (s u)").bitcast(BF16)
-            nc.vector.quantize_mx(codes[j][:, cols].bitcast(FP8X4), scales[j][:, cols], values)
+            nc.vector.quantize_mx(z_codes[j][:, cols].bitcast(FP8X4), z_bytes[j][:, cols], values)
+
+        whole = slice(0, S)
+        halves = [slice(0, S // 2), slice(S // 2, S)]
+        for t in range(PACK):
+            nc.scalar.copy(z_pairs[:, t // 2, :, t % 2], z_rows[t][:])
+        group(z_grouped, z_pairs, whole)
+        for t in range(PACK):
+            rounded, gain = z2_pairs[:, t // 2, :, t % 2], gm_rows[:, t : t + 1]
+            if t < 2:
+                nc.scalar.activation(rounded, z2_rows[t][:], ACT.Copy, scale=gain)
+            else:
+                nc.vector.tensor_scalar(rounded, z2_rows[t][:], gain, None, ALU.mult)
+        quantize(0, z_grouped, whole)
+        for cols in halves:
+            group(z2_grouped, z2_pairs, cols)
+        for cols in halves:
+            quantize(1, z2_grouped, cols)
 
         def h_pass(j, t, cols, out):
             rows = slice(P * t, P * (t + 1))
             nc.tensor.matmul_mx(
                 out, lhsT=w_words[:, j, rows].bitcast(FP8X4), lhsT_scale=w_bytes[4 * j :, rows],
-                rhs=codes[j][:, cols].bitcast(FP8X4), rhs_scale=scales[j][:, cols], start=(j == 0), stop=(j == 1),
+                rhs=z_codes[j][:, cols].bitcast(FP8X4), rhs_scale=z_bytes[j][:, cols], start=(j == 0), stop=(j == 1),
             )
 
-        whole = slice(0, S)
-        halves = [slice(0, S // 2), slice(S // 2, S)]
-        z_grouped = keep.tile([P, S, 2], I32, name="z_grouped", align_bytes=64)
-        z2_grouped = keep.tile([P, S, 2], I32, name="z2_grouped", align_bytes=64)
-        round_z(PACK - 1)
-        nc.vector.tensor_copy(z_grouped[:], pair_words(z_pairs, I32, whole))
-        for t in range(PACK):
-            round_z2(t)
-        quantize(0, z_grouped, whole)
-        for cols in halves:
-            nc.vector.tensor_copy(z2_grouped[:, cols, :], pair_words(z2_pairs, I32, cols))
-        for cols in halves:
-            quantize(1, z2_grouped, cols)
         first_banks = [psum.tile([P, S // 2], F32, name="bank_h0_%d" % u, tag=("bank_a0", "bank_b0")[u]) for u in range(2)]
         for j in range(2):
             for u, cols in enumerate(halves):
                 h_pass(j, 0, cols, first_banks[u][:])
         nc.scalar.copy(h_rows[0][:, halves[0]], first_banks[0][:])
         nc.vector.tensor_copy(h_rows[0][:, halves[1]], first_banks[1][:])
-        for t in range(1, PACK):
-            bank = psum.tile([P, S], F32, name="bank_h%d" % t, tag=("bank_a1", "bank_a0", "bank_b0")[t - 1])
+        for t, tag in ((1, "bank_a1"), (2, "bank_a0"), (3, "bank_b0")):
+            bank = psum.tile([P, S], F32, name="bank_h%d" % t, tag=tag)
             for j in range(2):
                 h_pass(j, t, whole, bank[:])
-            nc.vector.tensor_copy(h_rows[t][:, :S], bank[:])
+            nc.vector.tensor_copy(h_rows[t][:, whole], bank[:])
 
         out_rows = out_0.rearrange("(p t) j -> p t j", t=PACK)
         out_words = words_in_hbm(out_1)
         out_bytes = keep.tile([P, S], U8, name="out_bytes", align_bytes=64)
-        def extreme_steps(c, u, largest):
+
+        def member_steps(c, u, largest):
             cols = slice(CHUNK * c, CHUNK * (c + 1))
-            offsets = n5_l[:, cols.start * MEMBERS // 16 : cols.stop * MEMBERS // 16]
+            offsets = n5_list[:, cols.start * MEMBERS // PER_COLUMN : cols.stop * MEMBERS // PER_COLUMN]
             members = work.tile([P, 2, CHUNK * MEMBERS], F32, name="members", tag="members%d" % u, bufs=1)
             for e in range(2):
                 nc.scalar.activation(members[:, e, :], h_rows[2 * u + e][:].indirect(offsets), ACT.Copy)
-            quads = members[:].rearrange("p e (j m) -> p (e j) m", m=MEMBERS)
-            pair_min = work.tile([P, 2 * CHUNK, 2], F32, name="pair_min")
-            pair_max = work.tile([P, 2 * CHUNK, 2], F32, name="pair_max")
+            fours = members[:].rearrange("p e (j m) -> p (e j) m", m=MEMBERS)
+            two_min = work.tile([P, 2 * CHUNK, 2], F32, name="two_min")
+            two_max = work.tile([P, 2 * CHUNK, 2], F32, name="two_max")
             smallest = work.tile([P, 2, CHUNK], F32, name="smallest")
             above = work.tile([P, 2, CHUNK], F32, name="above", tag=("above", "members1")[u], bufs=(2, 1)[u])
             flat = "p e j -> p (e j)"
             steps = [
-                lambda: nc.vector.tensor_tensor(pair_min[:], quads[:, :, 0:2], quads[:, :, 2:4], ALU.min),
-                lambda: nc.vector.tensor_tensor(pair_max[:], quads[:, :, 0:2], quads[:, :, 2:4], ALU.max),
-                lambda: nc.vector.tensor_tensor(smallest[:].rearrange(flat), pair_min[:, :, 0], pair_min[:, :, 1], ALU.min),
+                lambda: nc.vector.tensor_tensor(two_min[:], fours[:, :, 0:2], fours[:, :, 2:4], ALU.min),
+                lambda: nc.vector.tensor_tensor(two_max[:], fours[:, :, 0:2], fours[:, :, 2:4], ALU.max),
+                lambda: nc.vector.tensor_tensor(smallest[:].rearrange(flat), two_min[:, :, 0], two_min[:, :, 1], ALU.min),
                 lambda: nc.vector.tensor_tensor(
-                    largest[:, 2 * u : 2 * u + 2, :].rearrange(flat), pair_max[:, :, 0], pair_max[:, :, 1], ALU.max
+                    largest[:, 2 * u : 2 * u + 2, :].rearrange(flat), two_max[:, :, 0], two_max[:, :, 1], ALU.max
                 ),
                 lambda: nc.vector.tensor_tensor(above[:, 0, :], h_rows[2 * u][:, cols], smallest[:, 0, :], ALU.subtract),
                 lambda: nc.vector.tensor_tensor(above[:, 1, :], h_rows[2 * u + 1][:, cols], smallest[:, 1, :], ALU.subtract),
             ]
             return steps, above
 
-        def finish_steps(c, largest, above, groups):
+        def finish_steps(c, largest, above, tile_groups):
             cols = slice(CHUNK * c, CHUNK * (c + 1))
-            bent = work.tile([P, PACK, CHUNK], F32, name="bent")
+            tanh_above = work.tile([P, PACK, CHUNK], F32, name="tanh_above")
             result = work.tile([P, PACK, CHUNK], F32, name="result")
-            grouped = work.tile([P, CHUNK, PACK], BF16, name="grouped", align_bytes=64)
-            codes = work.tile([P, CHUNK], I32, name="codes", align_bytes=64)
+            out_grouped = work.tile([P, CHUNK, PACK], BF16, name="out_grouped", align_bytes=64)
+            out_codes = work.tile([P, CHUNK], I32, name="out_codes", align_bytes=64)
 
             def multiply():
                 for u in range(2):
-                    nc.scalar.activation(bent[:, 2 * u : 2 * u + 2, :], above[u][:], ACT.Tanh)
-                for tiles in groups:
-                    nc.vector.tensor_tensor(result[:, tiles, :], largest[:, tiles, :], bent[:, tiles, :], ALU.mult)
+                    nc.scalar.activation(tanh_above[:, 2 * u : 2 * u + 2, :], above[u][:], ACT.Tanh)
+                for tiles in tile_groups:
+                    nc.vector.tensor_tensor(result[:, tiles, :], largest[:, tiles, :], tanh_above[:, tiles, :], ALU.mult)
                 nc.sync.dma_start(out_rows[:, :, cols], result[:])
 
-            def regroup():
+            def round_and_group():
                 nc.vector.tensor_copy(
-                    grouped[:].rearrange("p (c i) t -> p c t i", i=4), result[:].rearrange("p t (c i) -> p c t i", i=4)
+                    out_grouped[:].rearrange("p (c i) t -> p c t i", i=4), result[:].rearrange("p t (c i) -> p c t i", i=4)
                 )
 
             def quantize_out():
-                nc.vector.quantize_mx(codes[:].bitcast(FP8X4), out_bytes[:, cols], grouped[:].rearrange("p j t -> p (j t)"))
-                nc.sync.dma_start(out_words[:, cols], codes[:])
+                values = out_grouped[:].rearrange("p j t -> p (j t)")
+                nc.vector.quantize_mx(out_codes[:].bitcast(FP8X4), out_bytes[:, cols], values)
+                nc.sync.dma_start(out_words[:, cols], out_codes[:])
 
-            return [multiply, regroup, quantize_out]
+            return [multiply, round_and_group, quantize_out]
 
+        chunks = S // CHUNK
         pending = []
-        for c in range(S // CHUNK):
+        for c in range(chunks):
             largest = work.tile([P, PACK, CHUNK], F32, name="largest")
-            steps, above_first = extreme_steps(c, 0, largest)
+            steps, above_first = member_steps(c, 0, largest)
             for place, step in enumerate(steps):
                 step()
                 if pending and place >= 1:
                     pending.pop(0)()
-            steps, above_second = extreme_steps(c, 1, largest)
+            steps, above_second = member_steps(c, 1, largest)
             for step in steps:
                 step()
-            last = c + 1 == S // CHUNK
-            groups = [slice(0, 2), slice(2, 4)] if last else [slice(0, PACK)]
-            pending = finish_steps(c, largest, (above_first, above_second), groups)
+            tile_groups = [slice(0, 2), slice(2, PACK)] if c + 1 == chunks else [slice(0, PACK)]
+            pending = finish_steps(c, largest, (above_first, above_second), tile_groups)
         for step in pending:
             step()
-        for q in range(4):
+        for q in range(QUADS):
             queue = nc.sync if q % 2 == 0 else nc.scalar
             queue.dma_start(out_2[0, 4 * q : 4 * q + 4, :].bitcast(I32), out_bytes[32 * q : 32 * q + 4, :].bitcast(I32))

from contextlib import ExitStack

import concourse.mybir as mybir

T, S, N, G, H, W = 1024, 512, 512, 2048, 512, 256
FLOPS = 4 * 2 * 512 * 512 * 512

F32 = mybir.dt.float32
BF16 = mybir.dt.bfloat16
I32 = mybir.dt.int32
U32 = mybir.dt.uint32
U16 = mybir.dt.uint16
U8 = mybir.dt.uint8
FP8X4 = mybir.dt.float8_e4m3fn_x4
ALU = mybir.AluOpType
ACT = mybir.ActivationFunctionType

P = 128
PACK = 4
QUADS = 4
PER_COLUMN = 16
MEMBERS = 4
CHUNK = 128
SPARE = 16
SCORE_SCALE = 0.0625


def tile_picked_kjduelminmxgtan_none_po_kernel(
    tc, x_words, x_scales, d_words, d_scales, gn, gm, w1_words, w1_scales, w2_words, w2_scales,
    offs, k1, two, n1, n2, n3, n4, n5, out_0, out_1, out_2,
):
    nc = tc.nc

    def words_in_hbm(words):
        return words[0].rearrange("p c r -> p (c r)").bitcast(I32)

    with ExitStack() as ctx:
        lists = ctx.enter_context(tc.tile_pool(name="lists", bufs=1))
        keep = ctx.enter_context(tc.tile_pool(name="keep", bufs=1))
        work = ctx.enter_context(tc.tile_pool(name="work", bufs=PACK))
        psum = ctx.enter_context(tc.psum_pool(name="psum", bufs=1))

        def load_list(source, name):
            tile = lists.tile(list(source.shape), U16, name=name)
            nc.sync.dma_start(tile[:], source)
            return tile

        def deal(out, in_):
            nc.vector.tensor_copy(out.rearrange("p (t m) -> p m t", t=PACK), in_.rearrange("p (m t) -> p m t", t=PACK))

        d_bytes = keep.tile([P, G], U8, name="d_bytes", align_bytes=64)
        x_bytes = keep.tile([P, T], U8, name="x_bytes", tag="bytes_in", align_bytes=64)
        nc.vector.memset(d_bytes[:].bitcast(I32), 0)
        nc.vector.memset(x_bytes[:].bitcast(I32), 0)
        k1_list = load_list(k1, "k1_list")
        offs_list = load_list(offs, "offs_list")
        for e in range(2):
            nc.sync.dma_start(d_bytes[e:P:16, :].bitcast(I32), d_scales[0, e:16:2, :].bitcast(I32))
        x_table = keep.tile([P, T], I32, name="x_table", align_bytes=64)
        nc.sync.dma_start(x_table[:], words_in_hbm(x_words))
        d_table = keep.tile([P, G], I32, name="d_table", tag="words_in", align_bytes=64)
        nc.sync.dma_start(d_table[:], words_in_hbm(d_words))
        for q in range(QUADS):
            nc.sync.dma_start(x_bytes[32 * q : 32 * q + 4, :].bitcast(I32), x_scales[0, 4 * q : 4 * q + 4, :].bitcast(I32))
        two_list = load_list(two, "two_list")
        n1_list = load_list(n1, "n1_list")
        n2_list = load_list(n2, "n2_list")
        n3_list = load_list(n3, "n3_list")
        n4_list = load_list(n4, "n4_list")
        n5_list = load_list(n5, "n5_list")
        gn_rows = keep.tile([P, PACK], F32, name="gn_rows")
        gm_rows = keep.tile([P, PACK], F32, name="gm_rows")
        nc.gpsimd.dma_start(gn_rows[:], gn.rearrange("(p t) o -> p (t o)", t=PACK))
        nc.gpsimd.dma_start(gm_rows[:], gm.rearrange("(p t) o -> p (t o)", t=PACK))

        h_rows = [keep.tile([P, S + SPARE], F32, name="h_rows%d" % t) for t in range(PACK)]
        for t in range(PACK):
            nc.gpsimd.memset(h_rows[t][:, S:], 0.0)

        picked_key_bytes = keep.tile([P, H], U8, name="picked_key_bytes", align_bytes=64)
        key_bytes = keep.tile([P, H], U8, name="key_bytes", align_bytes=64)
        nc.vector.tensor_copy(picked_key_bytes[:], d_bytes[:].indirect(k1_list[:]))
        deal(key_bytes[:], picked_key_bytes[:])
        for e in range(2):
            nc.scalar.dma_start(key_bytes[2 + e : P : 32, :].bitcast(I32), key_bytes[16 + e : P : 32, :].bitcast(I32))

        def pick_tokens(offsets, name):
            words = keep.tile([P, S], U32, name=name + "_words", align_bytes=64)
            scale_bytes = keep.tile([P, S], U8, name=name + "_bytes", align_bytes=64)
            nc.vector.tensor_copy(words[:], x_table[:].bitcast(U32).indirect(offsets[:]))
            nc.vector.tensor_copy(scale_bytes[:], x_bytes[:].indirect(offsets[:]))
            return words, scale_bytes

        a_tokens = pick_tokens(offs_list, "a_token")
        picked_key_words = keep.tile([P, H], U32, name="picked_key_words", align_bytes=64)
        key_words = keep.tile([P, H], U32, name="key_words", align_bytes=64)
        nc.vector.tensor_copy(picked_key_words[:], d_table[:].bitcast(U32).indirect(k1_list[:]))
        deal(key_words[:], picked_key_words[:])

        def score(words, scale_bytes, name):
            banks = []
            for t in range(PACK):
                bank = psum.tile([P, S], F32, name="%s%d" % (name, t))
                keys = slice(P * t, P * (t + 1))
                nc.tensor.matmul_mx(
                    bank[:], lhsT=key_words[:, keys].bitcast(FP8X4), lhsT_scale=key_bytes[:, keys],
                    rhs=words[:].bitcast(FP8X4), rhs_scale=scale_bytes[:], start=True, stop=True,
                )
                banks.append(bank)
            return banks

        a_banks = score(*a_tokens, "bank_a")
        b_banks = score(*pick_tokens(two_list, "b_token"), "bank_b")

        w_table = keep.tile([P, 2, N], I32, name="w_table", tag="words_in", align_bytes=64)
        nc.scalar.dma_start(w_table[:, 0, :], words_in_hbm(w1_words))
        nc.scalar.dma_start(w_table[:, 1, :], words_in_hbm(w2_words))
        loaded_w_bytes = keep.tile([P, N], U8, name="loaded_w_bytes", tag="bytes_in", align_bytes=64)
        nc.gpsimd.memset(loaded_w_bytes[:].bitcast(I32), 0)
        for j, w_scales in enumerate((w1_scales, w2_scales)):
            for q in range(QUADS):
                rows = slice(32 * q + 4 * j, 32 * q + 4 * j + 4)
                nc.sync.dma_start(loaded_w_bytes[rows, :].bitcast(I32), w_scales[0, 4 * q : 4 * q + 4, :].bitcast(I32))

        half_gn = keep.tile([P, 2, PACK], F32, name="half_gn")
        nc.scalar.activation(half_gn[:, 0, :], gn_rows[:], ACT.Copy, scale=-0.5)
        nc.scalar.activation(half_gn[:, 1, :], gn_rows[:], ACT.Copy, scale=0.5)

        a_tags = ("a_rows", "a_rows", "gap0", "a_rows")
        b_tags = ("gap1", "gap2", "gap3", "gap0")

        def empty_bank(bank, tag):
            rows = work.tile([P, S], F32, name="score_rows", tag=tag, bufs=1)
            nc.scalar.activation(rows[:], bank[:], ACT.Copy, scale=SCORE_SCALE)
            return rows

        def pick_pairs(t, a_rows):
            pa = work.tile([P, W], F32, name="pa")
            pb = work.tile([P, W], F32, name="pb")
            nc.scalar.activation(pa[:], a_rows[:].indirect(n1_list[:]), ACT.Copy)
            nc.scalar.activation(pb[:], a_rows[:].indirect(n2_list[:]), ACT.Copy)
            gap = work.tile([P, W], F32, name="gap", tag="gap%d" % t, bufs=1)
            nc.vector.tensor_tensor(gap[:], pb[:], pa[:], ALU.subtract)
            return pa, pb, gap

        def put_pairs(t, pa, pb, gap):
            tanh_gap = work.tile([P, W], F32, name="tanh_gap")
            nc.scalar.activation(tanh_gap[:], gap[:], ACT.Tanh, scale=0.5)
            factor_a = work.tile([P, W], F32, name="factor_a")
            factor_b = work.tile([P, W], F32, name="factor_b")
            minus, plus = half_gn[:, 0, t : t + 1], half_gn[:, 1, t : t + 1]
            nc.vector.tensor_scalar(factor_a[:], tanh_gap[:], minus, plus, ALU.mult, ALU.add)
            nc.vector.tensor_scalar(factor_b[:], tanh_gap[:], plus, plus, ALU.mult, ALU.add)
            rows = work.tile([P, S], F32, name="z_rows")
            nc.vector.tensor_tensor(rows[:].indirect(n1_list[:]), pa[:], factor_a[:], ALU.mult)
            nc.vector.tensor_tensor(rows[:].indirect(n2_list[:]), pb[:], factor_b[:], ALU.mult)
            return rows

        def larger_of(t, b_rows):
            at_n3 = work.tile([P, S], F32, name="at_n3", tag="at_n3_%d" % t, bufs=1)
            at_n4 = work.tile([P, S], F32, name="at_n4")
            for picked, offsets in ((at_n3, n3_list), (at_n4, n4_list)):
                for u in range(2):
                    half_list = offsets[:, W // PER_COLUMN * u : W // PER_COLUMN * (u + 1)]
                    nc.scalar.activation(picked[:, W * u : W * (u + 1)], b_rows[:].indirect(half_list), ACT.Copy)
            larger = work.tile([P, S], F32, name="larger")
            nc.vector.tensor_tensor(larger[:], b_rows[:], at_n3[:], ALU.max)
            return larger, at_n4

        def smaller_of(larger, at_n4, tag):
            smaller = work.tile([P, S], F32, name="smaller", tag=tag, bufs=1)
            nc.vector.tensor_tensor(smaller[:], larger[:], at_n4[:], ALU.min)
            return smaller

        w_words = keep.tile([P, 2, N], I32, name="w_words", align_bytes=64)
        w_bytes = keep.tile([P, N], U8, name="w_bytes", align_bytes=64)
        for j in range(2):
            deal(w_words[:, j, :], w_table[:, j, :])

        pairs = [pick_pairs(0, empty_bank(a_banks[0], a_tags[0]))]
        a_rows_1 = empty_bank(a_banks[1], a_tags[1])
        z_rows = [put_pairs(0, *pairs[0])]
        pairs.append(pick_pairs(1, a_rows_1))
        a_rows_2 = empty_bank(a_banks[2], a_tags[2])
        a_rows_3 = empty_bank(a_banks[3], a_tags[3])
        pairs.append(pick_pairs(2, a_rows_2))
        z_rows.append(put_pairs(1, *pairs[1]))
        pairs.append(pick_pairs(3, a_rows_3))
        deal(w_bytes[:], loaded_w_bytes[:])
        compared, z2_rows = [], []
        for t in range(PACK):
            b_rows = empty_bank(b_banks[t], b_tags[t])
            if t + 2 < PACK:
                z_rows.append(put_pairs(t + 2, *pairs[t + 2]))
            compared.append(larger_of(t, b_rows))
            if t + 2 < PACK:
                z2_rows.append(smaller_of(*compared[t], "smaller%d" % t))
        z2_rows.append(smaller_of(*compared[2], "at_n3_3"))
        z2_rows.append(smaller_of(*compared[3], "smaller3"))

        z_pairs = keep.tile([P, 2, S, 2], BF16, name="z_pairs", align_bytes=64)
        z2_pairs = keep.tile([P, 2, S, 2], BF16, name="z2_pairs", align_bytes=64)
        z_grouped = keep.tile([P, S, 2], I32, name="z_grouped", align_bytes=64)
        z2_grouped = keep.tile([P, S, 2], I32, name="z2_grouped", align_bytes=64)
        z_codes = [keep.tile([P, S], U32, name="z_codes%d" % j, align_bytes=64) for j in range(2)]
        z_bytes = [keep.tile([P, S], U8, name="z_bytes%d" % j, align_bytes=64) for j in range(2)]

        def group(grouped, rounded, cols):
            words = rounded[:].rearrange("p u s e -> p u (s e)").bitcast(I32)
            nc.vector.tensor_copy(grouped[:, cols, :], words[:, :, cols].rearrange("p u s -> p s u"))

        def quantize(j, grouped, cols):
            values = grouped[:, cols, :].rearrange("p s u -> p (s u)").bitcast(BF16)
            nc.vector.quantize_mx(z_codes[j][:, cols].bitcast(FP8X4), z_bytes[j][:, cols], values)

        whole = slice(0, S)
        halves = [slice(0, S // 2), slice(S // 2, S)]
        for t in range(PACK):
            nc.scalar.copy(z_pairs[:, t // 2, :, t % 2], z_rows[t][:])
        group(z_grouped, z_pairs, whole)
        for t in range(PACK):
            rounded, gain = z2_pairs[:, t // 2, :, t % 2], gm_rows[:, t : t + 1]
            if t < 2:
                nc.scalar.activation(rounded, z2_rows[t][:], ACT.Copy, scale=gain)
            else:
                nc.vector.tensor_scalar(rounded, z2_rows[t][:], gain, None, ALU.mult)
        quantize(0, z_grouped, whole)
        for cols in halves:
            group(z2_grouped, z2_pairs, cols)
        for cols in halves:
            quantize(1, z2_grouped, cols)

        def h_pass(j, t, cols, out):
            rows = slice(P * t, P * (t + 1))
            nc.tensor.matmul_mx(
                out, lhsT=w_words[:, j, rows].bitcast(FP8X4), lhsT_scale=w_bytes[4 * j :, rows],
                rhs=z_codes[j][:, cols].bitcast(FP8X4), rhs_scale=z_bytes[j][:, cols], start=(j == 0), stop=(j == 1),
            )

        first_banks = [psum.tile([P, S // 2], F32, name="bank_h0_%d" % u, tag=("bank_a0", "bank_b0")[u]) for u in range(2)]
        for j in range(2):
            for u, cols in enumerate(halves):
                h_pass(j, 0, cols, first_banks[u][:])
        nc.scalar.copy(h_rows[0][:, halves[0]], first_banks[0][:])
        nc.vector.tensor_copy(h_rows[0][:, halves[1]], first_banks[1][:])
        for t, tag in ((1, "bank_a1"), (2, "bank_a0"), (3, "bank_b0")):
            bank = psum.tile([P, S], F32, name="bank_h%d" % t, tag=tag)
            for j in range(2):
                h_pass(j, t, whole, bank[:])
            nc.vector.tensor_copy(h_rows[t][:, whole], bank[:])

        out_rows = out_0.rearrange("(p t) j -> p t j", t=PACK)
        out_words = words_in_hbm(out_1)
        out_bytes = keep.tile([P, S], U8, name="out_bytes", align_bytes=64)

        def member_steps(c, u, largest):
            cols = slice(CHUNK * c, CHUNK * (c + 1))
            offsets = n5_list[:, cols.start * MEMBERS // PER_COLUMN : cols.stop * MEMBERS // PER_COLUMN]
            members = work.tile([P, 2, CHUNK * MEMBERS], F32, name="members", tag="members%d" % u, bufs=1)
            for e in range(2):
                nc.scalar.activation(members[:, e, :], h_rows[2 * u + e][:].indirect(offsets), ACT.Copy)
            fours = members[:].rearrange("p e (j m) -> p (e j) m", m=MEMBERS)
            two_min = work.tile([P, 2 * CHUNK, 2], F32, name="two_min")
            two_max = work.tile([P, 2 * CHUNK, 2], F32, name="two_max")
            smallest = work.tile([P, 2, CHUNK], F32, name="smallest")
            above = work.tile([P, 2, CHUNK], F32, name="above", tag=("above", "members1")[u], bufs=(2, 1)[u])
            flat = "p e j -> p (e j)"
            steps = [
                lambda: nc.vector.tensor_tensor(two_min[:], fours[:, :, 0:2], fours[:, :, 2:4], ALU.min),
                lambda: nc.vector.tensor_tensor(two_max[:], fours[:, :, 0:2], fours[:, :, 2:4], ALU.max),
                lambda: nc.vector.tensor_tensor(smallest[:].rearrange(flat), two_min[:, :, 0], two_min[:, :, 1], ALU.min),
                lambda: nc.vector.tensor_tensor(
                    largest[:, 2 * u : 2 * u + 2, :].rearrange(flat), two_max[:, :, 0], two_max[:, :, 1], ALU.max
                ),
                lambda: nc.vector.tensor_tensor(above[:, 0, :], h_rows[2 * u][:, cols], smallest[:, 0, :], ALU.subtract),
                lambda: nc.vector.tensor_tensor(above[:, 1, :], h_rows[2 * u + 1][:, cols], smallest[:, 1, :], ALU.subtract),
            ]
            return steps, above

        def finish_steps(c, largest, above, tile_groups):
            cols = slice(CHUNK * c, CHUNK * (c + 1))
            tanh_above = work.tile([P, PACK, CHUNK], F32, name="tanh_above")
            result = work.tile([P, PACK, CHUNK], F32, name="result")
            out_grouped = work.tile([P, CHUNK, PACK], BF16, name="out_grouped", align_bytes=64)
            out_codes = work.tile([P, CHUNK], I32, name="out_codes", align_bytes=64)

            def multiply():
                for u in range(2):
                    nc.scalar.activation(tanh_above[:, 2 * u : 2 * u + 2, :], above[u][:], ACT.Tanh)
                for tiles in tile_groups:
                    nc.vector.tensor_tensor(result[:, tiles, :], largest[:, tiles, :], tanh_above[:, tiles, :], ALU.mult)
                nc.sync.dma_start(out_rows[:, :, cols], result[:])

            def round_and_group():
                nc.vector.tensor_copy(
                    out_grouped[:].rearrange("p (c i) t -> p c t i", i=4), result[:].rearrange("p t (c i) -> p c t i", i=4)
                )

            def quantize_out():
                values = out_grouped[:].rearrange("p j t -> p (j t)")
                nc.vector.quantize_mx(out_codes[:].bitcast(FP8X4), out_bytes[:, cols], values)
                nc.sync.dma_start(out_words[:, cols], out_codes[:])

            return [multiply, round_and_group, quantize_out]

        chunks = S // CHUNK
        pending = []
        for c in range(chunks):
            largest = work.tile([P, PACK, CHUNK], F32, name="largest")
            steps, above_first = member_steps(c, 0, largest)
            for place, step in enumerate(steps):
                step()
                if pending and place >= 1:
                    pending.pop(0)()
            steps, above_second = member_steps(c, 1, largest)
            for step in steps:
                step()
            tile_groups = [slice(0, 2), slice(2, PACK)] if c + 1 == chunks else [slice(0, PACK)]
            pending = finish_steps(c, largest, (above_first, above_second), tile_groups)
        for step in pending:
            step()
        for q in range(QUADS):
            queue = nc.sync if q % 2 == 0 else nc.scalar
            queue.dma_start(out_2[0, 4 * q : 4 * q + 4, :].bitcast(I32), out_bytes[32 * q : 32 * q + 4, :].bitcast(I32))
